import numpy as np
import ml_dtypes


def mxq(x, axis, fmt="e4m3"):
    dtype, down = {"e4m3": (ml_dtypes.float8_e4m3fn, 7), "e5m2": (ml_dtypes.float8_e5m2, 14)}[fmt]
    v = np.moveaxis(np.asarray(x, np.float32).astype(ml_dtypes.bfloat16).astype(np.float64), axis, -1)
    blocks = v.reshape(v.shape[:-1] + (-1, 32))
    amax = np.abs(blocks).max(-1, keepdims=True)
    byte = np.maximum(np.where(amax > 0, np.frexp(amax)[1] - 1 + 127, 0) - down, 1)
    scale = np.exp2(byte - 127.0)
    codes = (blocks / scale).astype(np.float32).astype(dtype).astype(np.float64)
    return np.moveaxis((codes * scale).reshape(v.shape), -1, axis)


WIDE = False


def mx_kscale(k):
    if not WIDE:
        return np.ones(k)
    levels = np.array([10, -10, 5, -5, 0])
    if k % 512:
        return np.exp2(np.random.permutation(np.resize(levels, k // 32))).repeat(32)
    a = np.empty((k // 512, 16))
    for p in range(k // 512):
        a[p, :8] = np.random.permutation(np.resize(levels, 8))
        for g in range(8):
            far = levels[np.abs(levels - a[p, g]) >= 10]
            a[p, g + 8] = far[np.random.randint(len(far))]
    return np.exp2(a.ravel()).repeat(32)


BF16 = ml_dtypes.bfloat16


def bf(x):
    return np.asarray(x, np.float32).astype(BF16)


def f64(x):
    return np.asarray(x).astype(np.float64)


E2M1 = np.array([0.0, 0.5, 1.0, 1.5, 2.0, 3.0, 4.0, 6.0, -0.0, -0.5, -1.0, -1.5, -2.0, -3.0, -4.0, -6.0])


def pack_weight(w, fmt):
    k, n = w.shape
    w = f64(bf(w)).reshape(k // 32, 32, n)
    amax = np.abs(w).max(1)
    if fmt == "e4m3":
        byte = np.frexp(amax)[1] - 1 + 127 - 7
    else:
        mant, ex = np.frexp(amax / 6.0)
        byte = np.where(mant > 0.5, ex, ex - 1) + 127
    byte = np.clip(np.where(amax > 0, byte, 1), 1, 254)
    scaled = (w * np.exp2(127.0 - byte)[:, None, :]).reshape(k, n).astype(np.float32)
    by_word = np.ascontiguousarray(scaled.reshape(k // 512, 128, 4, n).transpose(0, 1, 3, 2))
    if fmt == "e4m3":
        words = by_word.astype(ml_dtypes.float8_e4m3fn).view(np.uint8)
    else:
        c = by_word.astype(ml_dtypes.float4_e2m1fn).view(np.uint8) & 0xF
        words = c[..., 0::2] | (c[..., 1::2] << 4)
    return np.ascontiguousarray(words), np.ascontiguousarray(byte.astype(np.uint8).reshape(k // 512, 16, n))


def unpack_weight(words, scales, fmt):
    g, p, n, _ = words.shape
    if fmt == "e4m3":
        vals = np.ascontiguousarray(words).view(ml_dtypes.float8_e4m3fn).astype(np.float64)
    else:
        nib = np.empty((g, p, n, 4), np.uint8)
        nib[..., 0::2] = words & 0xF
        nib[..., 1::2] = words >> 4
        vals = E2M1[nib]
    vals = vals * np.repeat(np.exp2(scales.astype(np.float64) - 127.0), 8, axis=1)[..., None]
    return vals.transpose(0, 1, 3, 2).reshape(g * 512, n)
def pack4(w):
    words, scales = pack_weight(w, "e2m1")
    return words.reshape(words.shape[0], 128, -1), scales


def unpack4(words, scales):
    return unpack_weight(words.reshape(words.shape[0], 128, -1, 2), scales, "e2m1")


def planes(Y):
    n, m = Y.shape
    b = f64(bf(Y)).reshape(n // 32, 32, m)
    amax = np.abs(b).max(1)
    byte = np.clip(np.where(amax > 0, np.frexp(amax)[1] - 1 + 127 - 7, 1), 1, 254)
    codes = (b * np.exp2(127.0 - byte)[:, None, :]).reshape(n, m).astype(np.float32).astype(ml_dtypes.float8_e4m3fn).view(np.uint8)
    words = codes.reshape(n // 512, 128, 4, m).transpose(0, 1, 3, 2)
    return np.ascontiguousarray(words), np.ascontiguousarray(byte.astype(np.uint8).reshape(n // 512, 16, m))


L, V, B, D, P = 1024, 512, 2, 1024, 768

def setup_inputs():
    rn = np.random.randn
    s = mx_kscale(V)
    t = mx_kscale(D)
    S = rn(V, L) / np.sqrt(V) * s[:, None]
    E = (rn(V, B, D) * t).reshape(V, B * D) / s[:, None]
    scatter_words, scatter_scales = pack4(S)
    latent_words, latent_scales = pack4(E)
    return {
        "scatter_words": scatter_words, "scatter_scales": scatter_scales,
        "latent_words": latent_words, "latent_scales": latent_scales,
        "mask": bf(np.random.permutation(L) >= V),
        "mask_embedding": bf(0.8 * rn(D) * t),
        "head_weight": bf(rn(D, P) / np.sqrt(D) / t[:, None]),
        "head_bias": bf(0.4 * rn(P)),
        "target": bf(rn(L, B, P)),
        "patch_scale": bf(np.exp(0.8 * rn(L))),
    }

def reference(scatter_words, scatter_scales, latent_words, latent_scales, mask, mask_embedding,
              head_weight, head_bias, target, patch_scale):
    S = unpack4(scatter_words, scatter_scales)
    E = unpack4(latent_words, latent_scales)
    full = (S.T @ E).reshape(L, B, D)
    H = full + f64(mask)[:, None, None] * f64(mask_embedding)
    pred = (mxq(H.reshape(L * B, D), 1) @ mxq(f64(head_weight), 0)).reshape(L, B, P)
    y = (pred + f64(head_bias) - f64(target)) * f64(patch_scale)[:, None, None]
    Y = y.reshape(L, B * P)
    words, scales = planes(Y)
    return y, words, scales

@@ -1,0 +1,376 @@
+from contextlib import ExitStack
+
+import concourse.mybir as mybir
+from concourse.masks import make_identity
+
+L, V, B, D, C = 1024, 512, 2, 1024, 768
+FLOPS = 2 * V * L * B * D + 2 * L * B * D * C
+
+F32 = mybir.dt.float32
+BF16 = mybir.dt.bfloat16
+I32 = mybir.dt.int32
+U32 = mybir.dt.uint32
+U8 = mybir.dt.uint8
+FP8X4 = mybir.dt.float8_e4m3fn_x4
+FP4X4 = mybir.dt.float4_e2m1fn_x4
+ALU = mybir.AluOpType
+ACT = mybir.ActivationFunctionType
+
+P = 128
+GROUP = 512
+CH = 256
+UNITS = 4
+S_PLANE = B * D
+
+
+def tile_soft_scatter_pixel_error_k5_kernel(
+    tc, scatter_words, scatter_scales, latent_words, latent_scales, mask, mask_embedding,
+    head_weight, head_bias, target, patch_scale, out_0, out_1, out_2,
+):
+    nc = tc.nc
+    with ExitStack() as ctx:
+        keep = ctx.enter_context(tc.tile_pool(name="keep", bufs=1))
+        ring = ctx.enter_context(tc.tile_pool(name="ring", bufs=2))
+        psum = ctx.enter_context(tc.psum_pool(name="psum", bufs=1))
+        ctx.enter_context(tc.manual_schedule())
+
+        planes = keep.tile([P, S_PLANE + L], U8, align_bytes=64)
+        mask_rows = keep.tile([P, P], BF16)
+        ident = keep.tile([P, P], F32)
+        ident_bf = keep.tile([P, P], BF16)
+        emb_in = keep.tile([P, D // P], BF16)
+        bias_in = keep.tile([P, C // P], BF16)
+        scale_in = keep.tile([P, 2, 4], BF16)
+        s_words = keep.tile([P, 2 * L], U8, align_bytes=64)
+        e_words = [keep.tile([P, 2 * D], U8, align_bytes=64, name="e_words%d" % r) for r in range(B)]
+        w_raw = [keep.tile([P, 4, C], BF16, name="w_raw%d" % g) for g in range(2)]
+        w_in = [keep.tile([P, C, 4], BF16, align_bytes=64, name="w_in%d" % g) for g in range(2)]
+        w_codes = [keep.tile([P, C], U32, align_bytes=64, name="w_codes%d" % g) for g in range(2)]
+        w_scales = [keep.tile([P, C], U8, align_bytes=64, name="w_scales%d" % g) for g in range(2)]
+        tgt = [keep.tile([P, 4, C], BF16, name="tgt%d" % u) for u in range(UNITS)]
+        emb_all = keep.tile([P, D], BF16)
+        bias_all = keep.tile([P, C], BF16)
+        mask_col = keep.tile([P, L // P], F32)
+        scale_col = keep.tile([P, 8], F32)
+        y_scales = [keep.tile([P, B * C], U8, align_bytes=64, name="y_scales%d" % g) for g in range(2)]
+
+        def load_scale_rows(source, col0, width, q):
+            nc.sync.dma_start(
+                out=planes[32 * q : 32 * q + 4, col0 : col0 + width].bitcast(I32),
+                in_=source[0, 4 * q : 4 * q + 4, :].bitcast(I32),
+            )
+
+        def load_latents(r):
+            nc.sync.dma_start(
+                out=e_words[r][:].bitcast(I32),
+                in_=latent_words[0, :, 2 * D * r : 2 * D * (r + 1)].bitcast(I32),
+            )
+
+        def load_weight(engine, g):
+            rows = head_weight[GROUP * g : GROUP * (g + 1), :]
+            engine.dma_start(out=w_raw[g][:], in_=rows.rearrange("(p j) c -> p j c", j=4))
+
+        def load_target(u):
+            rows = target[GROUP * (u // 2) : GROUP * (u // 2 + 1)]
+            nc.sync.dma_start(out=tgt[u][:], in_=rows.rearrange("(p t) r c -> p t r c", t=4)[:, :, u % 2, :])
+
+        nc.vector.memset(planes[:].bitcast(I32), 0)
+        nc.vector.memset(mask_rows[:], 0.0)
+        make_identity(nc, ident[:])
+        nc.sync.dma_start(out=emb_in[:], in_=mask_embedding.rearrange("(p j) -> p j", p=P))
+        nc.sync.dma_start(out=s_words[:].bitcast(I32), in_=scatter_words[0].bitcast(I32))
+        load_latents(0)
+        nc.sync.dma_start(out=mask_rows[0 : L // P, :], in_=mask.rearrange("(i p) -> i p", p=P))
+        for q in range(3):
+            load_scale_rows(latent_scales, 0, S_PLANE, q)
+        load_weight(nc.scalar, 0)
+        load_scale_rows(latent_scales, 0, S_PLANE, 3)
+        for q in range(4):
+            load_scale_rows(scatter_scales, S_PLANE, L, q)
+        nc.gpsimd.dma_start(out=bias_in[:], in_=head_bias.rearrange("(p j) -> p j", p=P))
+        nc.gpsimd.dma_start(out=scale_in[:], in_=patch_scale.rearrange("(g p t) -> p g t", p=P, t=4))
+        load_target(0)
+        load_weight(nc.sync, 1)
+        load_latents(1)
+        for u in range(1, UNITS):
+            load_target(u)
+
+        nc.scalar.activation(out=ident_bf[:], in_=ident[:], func=ACT.Copy)
+
+        def spread(bank, source, words):
+            for w in range(words):
+                column = source[:].bitcast(F32)[:, w : w + 1]
+                nc.tensor.transpose(bank[:, P * w : P * (w + 1)], column.to_broadcast([P, P]), ident[:])
+
+        emb_bank = psum.tile([P, 512], F32, tag="t0")
+        spread(emb_bank, emb_in, 4)
+        nc.scalar.copy(
+            out=emb_all[:].bitcast(F32).rearrange("p (g u a b) -> p g u a b", g=2, u=2, b=2),
+            in_=emb_bank[:].rearrange("p (b u g a) -> p g u a b", b=2, u=2, g=2),
+        )
+        mask_bank = psum.tile([P, P], BF16, tag="t1")
+        nc.tensor.transpose(mask_bank[:], mask_rows[:], ident_bf[:])
+        nc.scalar.copy(out=mask_col[:], in_=mask_bank[:, 0 : L // P])
+
+        mix_banks, head_banks, h_rows, h_in, h_codes, h_scales = {}, {}, {}, {}, {}, {}
+        offs, ys, y_in, y_codes = {}, {}, {}, {}
+
+        def interleave_weight(copy, g, c):
+            cols = slice(CH * c, CH * (c + 1))
+            copy(
+                out=w_in[g][:, cols, :].rearrange("p (c i) j -> p c j i", i=4),
+                in_=w_raw[g][:, :, cols].rearrange("p j (c i) -> p c j i", i=4),
+            )
+
+        def quantize_weight(g):
+            for c0, c1 in ((0, 512), (512, C)):
+                nc.vector.quantize_mx(
+                    out=w_codes[g][:, c0:c1].bitcast(FP8X4),
+                    scales=w_scales[g][:, c0:c1],
+                    in_=w_in[g][:, c0:c1, :].rearrange("p c j -> p (c j)"),
+                )
+
+        def mix(m):
+            if m >= 8 * UNITS:
+                return
+            u, i, g = m // 8, m % 8 // 2, m % 2
+            l0 = GROUP * (u // 2) + P * i
+            d0 = GROUP * g
+            bank = psum.tile([P, 512], F32, tag="m%d" % (m % 3), name="mix_bank")
+            nc.tensor.matmul_mx(
+                out=bank[:],
+                lhsT=s_words[:, 2 * l0 : 2 * (l0 + P)].bitcast(FP4X4),
+                lhsT_scale=planes[:, S_PLANE + l0 : S_PLANE + l0 + P],
+                rhs=e_words[u % 2][:, 2 * d0 : 2 * (d0 + GROUP)].bitcast(FP4X4),
+                rhs_scale=planes[:, D * (u % 2) + d0 : D * (u % 2) + d0 + GROUP],
+                start=True,
+                stop=True,
+            )
+            mix_banks[m] = bank
+
+        def add_embedding(m):
+            u, i, g = m // 8, m % 8 // 2, m % 2
+            if g == 0:
+                h_rows[m // 2] = ring.tile([P, D], BF16, tag="h_rows", bufs=3, name="h_rows")
+            tile_col = 4 * (u // 2) + i
+            pairs = mix_banks[m][:].rearrange("p (a u e) -> p u a e", u=2, e=2)
+            for half in range(2):
+                cols = slice(256 * (2 * g + half), 256 * (2 * g + half + 1))
+                nc.vector.scalar_tensor_tensor(
+                    out=h_rows[m // 2][:, cols].rearrange("p (a e) -> p a e", e=2),
+                    in0=emb_all[:, cols].rearrange("p (a e) -> p a e", e=2),
+                    scalar=mask_col[:, tile_col : tile_col + 1],
+                    in1=pairs[:, half],
+                    op0=ALU.mult,
+                    op1=ALU.add,
+                )
+
+        turned = {}
+
+        def turn(step):
+            bank = psum.tile([P, 512], F32, tag="t%d" % (step % 2), name="turn_bank")
+            words = h_rows[step][:].bitcast(F32)
+            for k in range(4):
+                nc.tensor.transpose(bank[:, P * k : P * (k + 1)], words[:, P * k : P * (k + 1)], ident[:])
+            turned[step] = bank
+
+        def gather_turned(step):
+            u, i = step // 4, step % 4
+            if i == 0:
+                h_in[u] = keep.tile([P, 4096], BF16, tag="big%d" % (u % 2), align_bytes=64, name="h_in")
+            words = h_in[u][:].bitcast(F32).rearrange("p (g t i j u) -> p g t i j u", g=2, t=4, i=4, u=2)
+            nc.scalar.copy(
+                out=words[:, :, :, i],
+                in_=turned[step][:].rearrange("p (g u j t) -> p g t j u", g=2, u=2, t=4),
+            )
+
+        def quantize_h(u):
+            h_codes[u] = ring.tile([P, 2 * GROUP], U32, tag="h_codes", align_bytes=64, name="h_codes")
+            h_scales[u] = ring.tile([P, 2 * GROUP], U8, tag="h_scales", align_bytes=64, name="h_scales")
+            nc.vector.quantize_mx(out=h_codes[u][:].bitcast(FP8X4), scales=h_scales[u][:], in_=h_in[u][:])
+
+        def subtract_target(engine, k):
+            u, c = k // 3, k % 3
+            tag = "big%d" % (u % 2) if c == 2 else "off%d_%d" % (c, u % 2)
+            offs[k] = keep.tile([P, 4, CH], F32, tag=tag, align_bytes=64, name="off")
+            cols = slice(CH * c, CH * (c + 1))
+            engine.tensor_tensor(
+                out=offs[k][:],
+                in0=bias_all[:, cols].rearrange("p (o c) -> p o c", o=1).to_broadcast([P, 4, CH]),
+                in1=tgt[u][:, :, cols],
+                op=ALU.subtract,
+            )
+
+        def scale_offset(k):
+            g = k // 6
+            for t in range(4):
+                nc.scalar.activation(
+                    out=offs[k][:, t, :], in_=offs[k][:, t, :], func=ACT.Copy,
+                    scale=scale_col[:, 4 * g + t : 4 * g + t + 1],
+                )
+
+        def head(h):
+            k = h // 2
+            u, c = k // 3, k % 3
+            bank = psum.tile([P, 512], F32, tag="h%d" % (h % 3), name="head_bank")
+            cols = slice(CH * c, CH * (c + 1))
+            for side in range(2):
+                t = 2 * (h % 2) + side
+                for g in range(2):
+                    rows = slice(GROUP * g + P * t, GROUP * g + P * (t + 1))
+                    nc.tensor.matmul_mx(
+                        out=bank[:, CH * side : CH * (side + 1)],
+                        lhsT=h_codes[u][:, rows].bitcast(FP8X4),
+                        lhsT_scale=h_scales[u][:, rows],
+                        rhs=w_codes[g][:, cols].bitcast(FP8X4),
+                        rhs_scale=w_scales[g][:, cols],
+                        start=(g == 0),
+                        stop=(g == 1),
+                    )
+            head_banks[h] = bank
+
+        def finish(h):
+            k = h // 2
+            u, c = k // 3, k % 3
+            g, r = u // 2, u % 2
+            if h % 2 == 0:
+                ys[k] = ring.tile([P, 4, CH], F32, tag="y", bufs=4, name="y")
+            for side in range(2):
+                t = 2 * (h % 2) + side
+                nc.vector.scalar_tensor_tensor(
+                    out=ys[k][:, t, :],
+                    in0=head_banks[h][:, CH * side : CH * (side + 1)],
+                    scalar=scale_col[:, 4 * g + t : 4 * g + t + 1],
+                    in1=offs[k][:, t, :],
+                    op0=ALU.mult,
+                    op1=ALU.add,
+                )
+            if h % 2 == 1:
+                rows = out_0[GROUP * g : GROUP * (g + 1)].rearrange("(p t) r c -> p t r c", t=4)
+                nc.sync.dma_start(out=rows[:, :, r, CH * c : CH * (c + 1)], in_=ys[k][:])
+
+        def interleave_y(copy, k):
+            y_in[k] = ring.tile([P, CH, 4], BF16, tag="y_in", bufs=6, align_bytes=64, name="y_in")
+            copy(
+                out=y_in[k][:].rearrange("p (c i) t -> p c t i", i=4),
+                in_=ys[k][:].rearrange("p t (c i) -> p c t i", i=4),
+            )
+
+        def quantize_y(k):
+            u, c = k // 3, k % 3
+            if c == 0:
+                y_codes[u] = ring.tile([P, C], U32, tag="y_codes", align_bytes=64, name="y_codes")
+            col0 = C * (u % 2) + CH * c
+            nc.vector.quantize_mx(
+                out=y_codes[u][:, CH * c : CH * (c + 1)].bitcast(FP8X4),
+                scales=y_scales[u // 2][:, col0 : col0 + CH],
+                in_=y_in[k][:].rearrange("p c t -> p (c t)"),
+            )
+
+        def store_codes(u, c0, c1):
+            col0 = C * (u % 2)
+            words = out_1[u // 2].rearrange("p n t -> p (n t)")
+            nc.sync.dma_start(
+                out=words[:, 4 * (col0 + c0) : 4 * (col0 + c1)].bitcast(I32),
+                in_=y_codes[u][:, c0:c1].bitcast(I32),
+            )
+
+        def store_scales(g):
+            for q in range(4):
+                nc.sync.dma_start(
+                    out=out_2[g, 4 * q : 4 * q + 4, :].bitcast(I32),
+                    in_=y_scales[g][32 * q : 32 * q + 4, :].bitcast(I32),
+                )
+
+        def step(s):
+            for g in range(2):
+                add_embedding(2 * s + g)
+                mix(2 * s + g + 3)
+            turn(s)
+
+        for m in range(3):
+            mix(m)
+        bias_bank = psum.tile([P, 512], F32, tag="h0")
+        spread(bias_bank, bias_in, 3)
+        nc.scalar.copy(
+            out=bias_all[:].bitcast(F32).rearrange("p (q w) -> p q w", w=3),
+            in_=bias_bank[:, 0 : 3 * P].rearrange("p (w q) -> p q w", w=3),
+        )
+        subtract_target(nc.gpsimd, 0)
+        interleave_weight(nc.vector.tensor_copy, 0, 0)
+        interleave_weight(nc.vector.tensor_copy, 0, 1)
+        interleave_weight(nc.scalar.copy, 0, 2)
+        for i in range(4):
+            step(i)
+            gather_turned(i)
+            if i < 3:
+                interleave_weight(nc.scalar.copy, 1, i)
+        nc.scalar.copy(out=scale_col[:], in_=scale_in[:].rearrange("p g t -> p (g t)"))
+        quantize_weight(0)
+        subtract_target(nc.vector, 1)
+        quantize_weight(1)
+        quantize_h(0)
+
+        for u in range(UNITS - 1):
+            k = 3 * u
+            for j in range(2, 5):
+                subtract_target(nc.gpsimd, k + j)
+            head(2 * k)
+            if u > 0:
+                finish(2 * k - 2)
+            head(2 * k + 1)
+            if u > 0:
+                finish(2 * k - 1)
+                interleave_y(nc.scalar.copy, k - 1)
+            else:
+                scale_offset(0)
+            head(2 * k + 2)
+            scale_offset(k + 1)
+            for i in range(4):
+                step(4 * (u + 1) + i)
+                gather_turned(4 * (u + 1) + i)
+                if i == 1:
+                    scale_offset(k + 2)
+            for h in range(2 * k, 2 * k + 4):
+                finish(h)
+                if h < 2 * k + 3:
+                    head(h + 3)
+                if h == 2 * k + 1:
+                    interleave_y(nc.scalar.copy, k)
+                    scale_offset(k + 3)
+            interleave_y(nc.scalar.copy, k + 1)
+            if u > 0:
+                for c in range(3):
+                    quantize_y(k - 3 + c)
+                store_codes(u - 1, 0, C)
+            if u == 2:
+                store_scales(0)
+            quantize_h(u + 1)
+
+        subtract_target(nc.gpsimd, 11)
+        scale_offset(10)
+        head(18)
+        finish(16)
+        head(19)
+        finish(17)
+        head(20)
+        interleave_y(nc.scalar.copy, 8)
+        scale_offset(11)
+        for h in range(18, 22):
+            finish(h)
+            if h < 21:
+                head(h + 3)
+            if h % 2 == 1:
+                interleave_y(nc.scalar.copy, h // 2)
+        for k in range(6, 9):
+            quantize_y(k)
+        store_codes(2, 0, C)
+        finish(22)
+        finish(23)
+        quantize_y(9)
+        interleave_y(nc.vector.tensor_copy, 11)
+        quantize_y(10)
+        store_codes(3, 0, 2 * CH)
+        quantize_y(11)
+        store_codes(3, 2 * CH, C)
+        store_scales(1)

@@ -20,6 +20,7 @@ P = 128
 GROUP = 512
 CH = 256
 UNITS = 4
+PIECES = [(0, 0, 512), (0, 512, 512), (0, 1024, 512), (1, 0, 512), (1, 512, 512), (1, 1024, 256), (1, 1280, 256)]
 S_PLANE = B * D
 
 
@@ -35,6 +36,8 @@ def tile_soft_scatter_pixel_error_k5_kernel(
         ctx.enter_context(tc.manual_schedule())
 
         planes = keep.tile([P, S_PLANE + L], U8, align_bytes=64)
+        e_scales = keep.tile([P, B * D], U8, align_bytes=64)
+        e_raw = keep.tile([P, B * D // 2], I32)
         mask_rows = keep.tile([P, P], BF16)
         ident = keep.tile([P, P], F32)
         ident_bf = keep.tile([P, P], BF16)
@@ -42,78 +45,88 @@ def tile_soft_scatter_pixel_error_k5_kernel(
         bias_in = keep.tile([P, C // P], BF16)
         scale_in = keep.tile([P, 2, 4], BF16)
         s_words = keep.tile([P, 2 * L], U8, align_bytes=64)
-        e_words = [keep.tile([P, 2 * D], U8, align_bytes=64, name="e_words%d" % r) for r in range(B)]
+        e_words = keep.tile([P, 2 * B * D], U8, align_bytes=64)
         w_raw = [keep.tile([P, 4, C], BF16, name="w_raw%d" % g) for g in range(2)]
-        w_in = [keep.tile([P, C, 4], BF16, align_bytes=64, name="w_in%d" % g) for g in range(2)]
+        w_in = [keep.tile([P, C, 4], BF16, align_bytes=64, tag="w_in%d" % g, name="w_in") for g in range(2)]
         w_codes = [keep.tile([P, C], U32, align_bytes=64, name="w_codes%d" % g) for g in range(2)]
         w_scales = [keep.tile([P, C], U8, align_bytes=64, name="w_scales%d" % g) for g in range(2)]
-        tgt = [keep.tile([P, 4, C], BF16, name="tgt%d" % u) for u in range(UNITS)]
+        tgt = [keep.tile([P, 4, w], BF16, name="tgt%d" % k) for k, (g, c0, w) in enumerate(PIECES)]
         emb_all = keep.tile([P, D], BF16)
-        bias_all = keep.tile([P, C], BF16)
+        bias_all = keep.tile([P, C + 6 * 43], BF16)
         mask_col = keep.tile([P, L // P], F32)
         scale_col = keep.tile([P, 8], F32)
+        y_codes = [keep.tile([P, B * C], U32, align_bytes=64, name="y_codes%d" % g) for g in range(2)]
         y_scales = [keep.tile([P, B * C], U8, align_bytes=64, name="y_scales%d" % g) for g in range(2)]
 
-        def load_scale_rows(source, col0, width, q):
-            nc.sync.dma_start(
-                out=planes[32 * q : 32 * q + 4, col0 : col0 + width].bitcast(I32),
-                in_=source[0, 4 * q : 4 * q + 4, :].bitcast(I32),
-            )
+        def load_scale_rows(engine, source, col0, width):
+            for q in range(4):
+                engine.dma_start(
+                    out=planes[32 * q : 32 * q + 4, col0 : col0 + width].bitcast(I32),
+                    in_=source[0, 4 * q : 4 * q + 4, :].bitcast(I32),
+                )
 
-        def load_latents(r):
-            nc.sync.dma_start(
-                out=e_words[r][:].bitcast(I32),
-                in_=latent_words[0, :, 2 * D * r : 2 * D * (r + 1)].bitcast(I32),
-            )
+        def load_weight(g, u):
+            rows = head_weight[GROUP * g : GROUP * (g + 1), :].rearrange("(q u r e) c -> u q r (e c)", u=2, r=8, e=2)
+            nc.sync.dma_start(out=w_raw[g][:, 2 * u : 2 * u + 2, :].rearrange("p e c -> p (e c)"), in_=rows[u])
 
-        def load_weight(engine, g):
-            rows = head_weight[GROUP * g : GROUP * (g + 1), :]
-            engine.dma_start(out=w_raw[g][:], in_=rows.rearrange("(p j) c -> p j c", j=4))
+        def load_target(k, t0=0, t1=4):
+            g, c0, w = PIECES[k]
+            rows = target[GROUP * g : GROUP * (g + 1)].rearrange("(p t) r c -> p t (r c)", t=4)
+            nc.sync.dma_start(out=tgt[k][:, t0:t1, :], in_=rows[:, t0:t1, c0 : c0 + w])
 
-        def load_target(u):
-            rows = target[GROUP * (u // 2) : GROUP * (u // 2 + 1)]
-            nc.sync.dma_start(out=tgt[u][:], in_=rows.rearrange("(p t) r c -> p t r c", t=4)[:, :, u % 2, :])
-
-        nc.vector.memset(planes[:].bitcast(I32), 0)
-        nc.vector.memset(mask_rows[:], 0.0)
+        nc.vector.memset(planes[:, 0:S_PLANE].bitcast(I32), 0)
+        nc.vector.memset(planes[:, S_PLANE:].bitcast(I32), 0)
+        nc.gpsimd.memset(mask_rows[:], 0.0)
+        nc.gpsimd.dma_start(out=emb_in[:], in_=mask_embedding.rearrange("(p j) -> p j", p=P))
+        nc.gpsimd.dma_start(out=mask_rows[0 : L // P, :], in_=mask.rearrange("(i p) -> i p", p=P))
         make_identity(nc, ident[:])
-        nc.sync.dma_start(out=emb_in[:], in_=mask_embedding.rearrange("(p j) -> p j", p=P))
-        nc.sync.dma_start(out=s_words[:].bitcast(I32), in_=scatter_words[0].bitcast(I32))
-        load_latents(0)
-        nc.sync.dma_start(out=mask_rows[0 : L // P, :], in_=mask.rearrange("(i p) -> i p", p=P))
-        for q in range(3):
-            load_scale_rows(latent_scales, 0, S_PLANE, q)
-        load_weight(nc.scalar, 0)
-        load_scale_rows(latent_scales, 0, S_PLANE, 3)
-        for q in range(4):
-            load_scale_rows(scatter_scales, S_PLANE, L, q)
-        nc.gpsimd.dma_start(out=bias_in[:], in_=head_bias.rearrange("(p j) -> p j", p=P))
         nc.gpsimd.dma_start(out=scale_in[:], in_=patch_scale.rearrange("(g p t) -> p g t", p=P, t=4))
-        load_target(0)
-        load_weight(nc.sync, 1)
-        load_latents(1)
-        for u in range(1, UNITS):
-            load_target(u)
-
+        load_scale_rows(nc.scalar, latent_scales, 0, S_PLANE)
+        nc.sync.dma_start(out=bias_in[:], in_=head_bias.rearrange("(p j) -> p j", p=P))
+        nc.sync.dma_start(out=s_words[:].bitcast(I32), in_=scatter_words[0].bitcast(I32))
+        nc.sync.dma_start(out=e_raw[:], in_=latent_words[0].bitcast(I32))
+        load_weight(0, 0)
         nc.scalar.activation(out=ident_bf[:], in_=ident[:], func=ACT.Copy)
+        load_scale_rows(nc.scalar, scatter_scales, S_PLANE, L)
+        load_target(0, 0, 2)
+        load_weight(0, 1)
+        load_target(0, 2, 4)
+        load_weight(1, 0)
+        load_weight(1, 1)
+        for k in range(1, len(PIECES)):
+            load_target(k)
+
+        def sort_columns(out, source, run):
+            nc.vector.tensor_copy(
+                out=out.rearrange("p (g u q x) -> p g u q x", u=2, q=16, x=run),
+                in_=source.rearrange("p (g q u x) -> p g u q x", u=2, q=16, x=run),
+            )
 
         def spread(bank, source, words):
             for w in range(words):
                 column = source[:].bitcast(F32)[:, w : w + 1]
                 nc.tensor.transpose(bank[:, P * w : P * (w + 1)], column.to_broadcast([P, P]), ident[:])
 
-        emb_bank = psum.tile([P, 512], F32, tag="t0")
+        sort_columns(e_scales[:].bitcast(I32), planes[:, 0:S_PLANE].bitcast(I32), 4)
+        bias_bank = psum.tile([P, 512], F32, tag="h2")
+        spread(bias_bank, bias_in, 3)
+        bias_words = bias_all[:].bitcast(F32).rearrange("p (q w) -> p q w", w=3)
+        bias_turned = bias_bank[:, 0 : 3 * P].rearrange("p (w q) -> p q w", w=3)
+        nc.vector.tensor_copy(out=bias_words[:, 0:P, :], in_=bias_turned)
+        nc.vector.tensor_copy(out=bias_words[:, P : P + 43, :], in_=bias_turned[:, 0:43, :])
+        sort_columns(e_words[:].bitcast(I32), e_raw[:], 8)
+        emb_bank = psum.tile([P, 512], F32, tag="h0")
         spread(emb_bank, emb_in, 4)
-        nc.scalar.copy(
-            out=emb_all[:].bitcast(F32).rearrange("p (g u a b) -> p g u a b", g=2, u=2, b=2),
-            in_=emb_bank[:].rearrange("p (b u g a) -> p g u a b", b=2, u=2, g=2),
+        nc.vector.tensor_copy(
+            out=emb_all[:].bitcast(F32).rearrange("p (u q h w) -> p u q h w", u=2, h=2, w=4),
+            in_=emb_bank[:].rearrange("p (w q u h) -> p u q h w", w=4, u=2, h=2),
         )
-        mask_bank = psum.tile([P, P], BF16, tag="t1")
+        mask_bank = psum.tile([P, P], BF16, tag="h1")
         nc.tensor.transpose(mask_bank[:], mask_rows[:], ident_bf[:])
-        nc.scalar.copy(out=mask_col[:], in_=mask_bank[:, 0 : L // P])
+        nc.vector.tensor_copy(out=mask_col[:], in_=mask_bank[:, 0 : L // P])
 
         mix_banks, head_banks, h_rows, h_in, h_codes, h_scales = {}, {}, {}, {}, {}, {}
-        offs, ys, y_in, y_codes = {}, {}, {}, {}
+        offs, ys, y_in = {}, {}, {}
 
         def interleave_weight(copy, g, c):
             cols = slice(CH * c, CH * (c + 1))
@@ -130,19 +143,25 @@ def tile_soft_scatter_pixel_error_k5_kernel(
                     in_=w_in[g][:, c0:c1, :].rearrange("p c j -> p (c j)"),
                 )
 
+        taken = []
+
+        def stage_one_bank():
+            taken.append(psum.tile([P, 512], F32, tag="a%d" % (len(taken) % 5), name="stage_one_bank"))
+            return taken[-1]
+
         def mix(m):
             if m >= 8 * UNITS:
                 return
             u, i, g = m // 8, m % 8 // 2, m % 2
             l0 = GROUP * (u // 2) + P * i
-            d0 = GROUP * g
-            bank = psum.tile([P, 512], F32, tag="m%d" % (m % 3), name="mix_bank")
+            d0 = D * (u % 2) + GROUP * g
+            bank = stage_one_bank()
             nc.tensor.matmul_mx(
                 out=bank[:],
                 lhsT=s_words[:, 2 * l0 : 2 * (l0 + P)].bitcast(FP4X4),
                 lhsT_scale=planes[:, S_PLANE + l0 : S_PLANE + l0 + P],
-                rhs=e_words[u % 2][:, 2 * d0 : 2 * (d0 + GROUP)].bitcast(FP4X4),
-                rhs_scale=planes[:, D * (u % 2) + d0 : D * (u % 2) + d0 + GROUP],
+                rhs=e_words[:, 2 * d0 : 2 * (d0 + GROUP)].bitcast(FP4X4),
+                rhs_scale=e_scales[:, d0 : d0 + GROUP],
                 start=True,
                 stop=True,
             )
@@ -151,24 +170,22 @@ def tile_soft_scatter_pixel_error_k5_kernel(
         def add_embedding(m):
             u, i, g = m // 8, m % 8 // 2, m % 2
             if g == 0:
-                h_rows[m // 2] = ring.tile([P, D], BF16, tag="h_rows", bufs=3, name="h_rows")
+                h_rows[m // 2] = ring.tile([P, D], BF16, tag="h_rows", bufs=4, name="h_rows")
             tile_col = 4 * (u // 2) + i
-            pairs = mix_banks[m][:].rearrange("p (a u e) -> p u a e", u=2, e=2)
-            for half in range(2):
-                cols = slice(256 * (2 * g + half), 256 * (2 * g + half + 1))
-                nc.vector.scalar_tensor_tensor(
-                    out=h_rows[m // 2][:, cols].rearrange("p (a e) -> p a e", e=2),
-                    in0=emb_all[:, cols].rearrange("p (a e) -> p a e", e=2),
-                    scalar=mask_col[:, tile_col : tile_col + 1],
-                    in1=pairs[:, half],
-                    op0=ALU.mult,
-                    op1=ALU.add,
-                )
+            cols = slice(GROUP * g, GROUP * (g + 1))
+            nc.vector.scalar_tensor_tensor(
+                out=h_rows[m // 2][:, cols].rearrange("p (u x) -> p u x", u=2),
+                in0=emb_all[:].rearrange("p (u g x) -> p u g x", u=2, g=2)[:, :, g, :],
+                scalar=mask_col[:, tile_col : tile_col + 1],
+                in1=mix_banks[m][:].rearrange("p (u x) -> p u x", u=2),
+                op0=ALU.mult,
+                op1=ALU.add,
+            )
 
         turned = {}
 
         def turn(step):
-            bank = psum.tile([P, 512], F32, tag="t%d" % (step % 2), name="turn_bank")
+            bank = stage_one_bank()
             words = h_rows[step][:].bitcast(F32)
             for k in range(4):
                 nc.tensor.transpose(bank[:, P * k : P * (k + 1)], words[:, P * k : P * (k + 1)], ident[:])
@@ -177,7 +194,7 @@ def tile_soft_scatter_pixel_error_k5_kernel(
         def gather_turned(step):
             u, i = step // 4, step % 4
             if i == 0:
-                h_in[u] = keep.tile([P, 4096], BF16, tag="big%d" % (u % 2), align_bytes=64, name="h_in")
+                h_in[u] = keep.tile([P, 4096], BF16, tag="big%d" % u, align_bytes=64, name="h_in")
             words = h_in[u][:].bitcast(F32).rearrange("p (g t i j u) -> p g t i j u", g=2, t=4, i=4, u=2)
             nc.scalar.copy(
                 out=words[:, :, :, i],
@@ -189,188 +206,201 @@ def tile_soft_scatter_pixel_error_k5_kernel(
             h_scales[u] = ring.tile([P, 2 * GROUP], U8, tag="h_scales", align_bytes=64, name="h_scales")
             nc.vector.quantize_mx(out=h_codes[u][:].bitcast(FP8X4), scales=h_scales[u][:], in_=h_in[u][:])
 
-        def subtract_target(engine, k):
-            u, c = k // 3, k % 3
-            tag = "big%d" % (u % 2) if c == 2 else "off%d_%d" % (c, u % 2)
-            offs[k] = keep.tile([P, 4, CH], F32, tag=tag, align_bytes=64, name="off")
-            cols = slice(CH * c, CH * (c + 1))
+        def place(j):
+            k = j // 2 if j < 10 else j - 5
+            slots = range(2 * (j % 2), 2 * (j % 2) + 2) if j < 10 else range(4)
+            return k, slots
+
+        def subtract_target(engine, j, tag):
+            k, slots = place(j)
+            g, c0, w = PIECES[k]
+            offs[j] = keep.tile([P, len(slots), w], F32, tag=tag, align_bytes=64, name="off")
             engine.tensor_tensor(
-                out=offs[k][:],
-                in0=bias_all[:, cols].rearrange("p (o c) -> p o c", o=1).to_broadcast([P, 4, CH]),
-                in1=tgt[u][:, :, cols],
+                out=offs[j][:],
+                in0=bias_all[:, c0 % C : c0 % C + w].rearrange("p (o c) -> p o c", o=1).to_broadcast([P, len(slots), w]),
+                in1=tgt[k][:, slots.start : slots.stop, :],
                 op=ALU.subtract,
             )
 
-        def scale_offset(k):
-            g = k // 6
-            for t in range(4):
+        def scale_offset(j):
+            k, slots = place(j)
+            g = PIECES[k][0]
+            for s, t in enumerate(slots):
                 nc.scalar.activation(
-                    out=offs[k][:, t, :], in_=offs[k][:, t, :], func=ACT.Copy,
+                    out=offs[j][:, s, :], in_=offs[j][:, s, :], func=ACT.Copy,
                     scale=scale_col[:, 4 * g + t : 4 * g + t + 1],
                 )
 
-        def head(h):
-            k = h // 2
-            u, c = k // 3, k % 3
-            bank = psum.tile([P, 512], F32, tag="h%d" % (h % 3), name="head_bank")
-            cols = slice(CH * c, CH * (c + 1))
-            for side in range(2):
-                t = 2 * (h % 2) + side
-                for g in range(2):
-                    rows = slice(GROUP * g + P * t, GROUP * g + P * (t + 1))
-                    nc.tensor.matmul_mx(
-                        out=bank[:, CH * side : CH * (side + 1)],
-                        lhsT=h_codes[u][:, rows].bitcast(FP8X4),
-                        lhsT_scale=h_scales[u][:, rows],
-                        rhs=w_codes[g][:, cols].bitcast(FP8X4),
-                        rhs_scale=w_scales[g][:, cols],
-                        start=(g == 0),
-                        stop=(g == 1),
-                    )
-            head_banks[h] = bank
+        def bank_slots(n):
+            k, slots = place(n // 2)
+            each = len(slots) // 2
+            return k, range(each * (n % 2), each * (n % 2 + 1)), slots
 
-        def finish(h):
-            k = h // 2
-            u, c = k // 3, k % 3
-            g, r = u // 2, u % 2
-            if h % 2 == 0:
-                ys[k] = ring.tile([P, 4, CH], F32, tag="y", bufs=4, name="y")
-            for side in range(2):
-                t = 2 * (h % 2) + side
+        def head(n):
+            k, local, slots = bank_slots(n)
+            g, c0, w = PIECES[k]
+            bank = psum.tile([P, 512], F32, tag="h%d" % (n % 3), name="head_bank")
+            at = 0
+            for s in local:
+                t = slots[s]
+                cuts = [c0, C, c0 + w] if c0 < C < c0 + w else [c0, c0 + w]
+                for a, b in zip(cuts, cuts[1:]):
+                    u = 2 * g + a // C
+                    cols = slice(a % C, a % C + b - a)
+                    for half in range(2):
+                        rows = slice(GROUP * half + P * t, GROUP * half + P * (t + 1))
+                        nc.tensor.matmul_mx(
+                            out=bank[:, at : at + b - a],
+                            lhsT=h_codes[u][:, rows].bitcast(FP8X4),
+                            lhsT_scale=h_scales[u][:, rows],
+                            rhs=w_codes[half][:, cols].bitcast(FP8X4),
+                            rhs_scale=w_scales[half][:, cols],
+                            start=(half == 0),
+                            stop=(half == 1),
+                        )
+                    at += b - a
+            head_banks[n] = bank
+
+        def finish(n):
+            j = n // 2
+            k, local, slots = bank_slots(n)
+            g, c0, w = PIECES[k]
+            if k not in ys:
+                ys[k] = ring.tile([P, 4, w], F32, tag="y", bufs=4, name="y")
+            for at, s in enumerate(local):
+                t = slots[s]
                 nc.vector.scalar_tensor_tensor(
                     out=ys[k][:, t, :],
-                    in0=head_banks[h][:, CH * side : CH * (side + 1)],
+                    in0=head_banks[n][:, w * at : w * (at + 1)],
                     scalar=scale_col[:, 4 * g + t : 4 * g + t + 1],
-                    in1=offs[k][:, t, :],
+                    in1=offs[j][:, s, :],
                     op0=ALU.mult,
                     op1=ALU.add,
                 )
-            if h % 2 == 1:
-                rows = out_0[GROUP * g : GROUP * (g + 1)].rearrange("(p t) r c -> p t r c", t=4)
-                nc.sync.dma_start(out=rows[:, :, r, CH * c : CH * (c + 1)], in_=ys[k][:])
+            if n % 2 == 1:
+                rows = out_0[GROUP * g : GROUP * (g + 1)].rearrange("(p t) r c -> p t (r c)", t=4)
+                nc.sync.dma_start(
+                    out=rows[:, slots.start : slots.stop, c0 : c0 + w], in_=ys[k][:, slots.start : slots.stop, :]
+                )
 
-        def interleave_y(copy, k):
-            y_in[k] = ring.tile([P, CH, 4], BF16, tag="y_in", bufs=6, align_bytes=64, name="y_in")
+        def interleave_y(copy, k, a, b):
+            if k not in y_in:
+                tag = "y_in%d" % k
+                y_in[k] = keep.tile([P, PIECES[k][2], 4], BF16, tag=tag, align_bytes=64, name="y_in")
             copy(
-                out=y_in[k][:].rearrange("p (c i) t -> p c t i", i=4),
-                in_=ys[k][:].rearrange("p t (c i) -> p c t i", i=4),
+                out=y_in[k][:, a:b, :].rearrange("p (c i) t -> p c t i", i=4),
+                in_=ys[k][:, :, a:b].rearrange("p t (c i) -> p c t i", i=4),
             )
 
-        def quantize_y(k):
-            u, c = k // 3, k % 3
-            if c == 0:
-                y_codes[u] = ring.tile([P, C], U32, tag="y_codes", align_bytes=64, name="y_codes")
-            col0 = C * (u % 2) + CH * c
+        def quantize_y(k, a, b):
+            g, c0, w = PIECES[k]
             nc.vector.quantize_mx(
-                out=y_codes[u][:, CH * c : CH * (c + 1)].bitcast(FP8X4),
-                scales=y_scales[u // 2][:, col0 : col0 + CH],
-                in_=y_in[k][:].rearrange("p c t -> p (c t)"),
+                out=y_codes[g][:, c0 + a : c0 + b].bitcast(FP8X4),
+                scales=y_scales[g][:, c0 + a : c0 + b],
+                in_=y_in[k][:, a:b, :].rearrange("p c t -> p (c t)"),
             )
 
-        def store_codes(u, c0, c1):
-            col0 = C * (u % 2)
-            words = out_1[u // 2].rearrange("p n t -> p (n t)")
-            nc.sync.dma_start(
-                out=words[:, 4 * (col0 + c0) : 4 * (col0 + c1)].bitcast(I32),
-                in_=y_codes[u][:, c0:c1].bitcast(I32),
-            )
+        def store_codes(g, a, b):
+            words = out_1[g].rearrange("p n t -> p (n t)")
+            nc.sync.dma_start(out=words[:, 4 * a : 4 * b].bitcast(I32), in_=y_codes[g][:, a:b].bitcast(I32))
 
         def store_scales(g):
             for q in range(4):
-                nc.sync.dma_start(
+                engine = nc.scalar if g == 1 and q % 2 else nc.sync
+                engine.dma_start(
                     out=out_2[g, 4 * q : 4 * q + 4, :].bitcast(I32),
                     in_=y_scales[g][32 * q : 32 * q + 4, :].bitcast(I32),
                 )
 
-        def step(s):
-            for g in range(2):
-                add_embedding(2 * s + g)
-                mix(2 * s + g + 3)
-            turn(s)
+        def il(k, half):
+            return lambda: interleave_y(nc.scalar.copy, k, CH * half, CH * (half + 1))
 
-        for m in range(3):
-            mix(m)
-        bias_bank = psum.tile([P, 512], F32, tag="h0")
-        spread(bias_bank, bias_in, 3)
-        nc.scalar.copy(
-            out=bias_all[:].bitcast(F32).rearrange("p (q w) -> p q w", w=3),
-            in_=bias_bank[:, 0 : 3 * P].rearrange("p (w q) -> p q w", w=3),
-        )
-        subtract_target(nc.gpsimd, 0)
-        interleave_weight(nc.vector.tensor_copy, 0, 0)
-        interleave_weight(nc.vector.tensor_copy, 0, 1)
-        interleave_weight(nc.scalar.copy, 0, 2)
-        for i in range(4):
-            step(i)
-            gather_turned(i)
-            if i < 3:
-                interleave_weight(nc.scalar.copy, 1, i)
-        nc.scalar.copy(out=scale_col[:], in_=scale_in[:].rearrange("p g t -> p (g t)"))
-        quantize_weight(0)
-        subtract_target(nc.vector, 1)
-        quantize_weight(1)
+        def so(j):
+            return lambda: scale_offset(j)
+
+        def iw(g, c):
+            return lambda: interleave_weight(nc.scalar.copy, g, c)
+
+        def stage_one(first, last, ahead_to, n0, jobs, head_at=()):
+            for m in range(first, last):
+                if n0 is not None and m - first in head_at:
+                    head(n0 + head_at.index(m - first))
+                add_embedding(m)
+                if m + 3 < ahead_to:
+                    mix(m + 3)
+                if m % 2:
+                    for job in jobs.get(m // 2, ()):
+                        job()
+                    turn(m // 2)
+                    gather_turned(m // 2)
+
+        def prefill(first):
+            for m in range(first, first + 3):
+                mix(m)
+
+        def drain(n0, n1, u, jobs):
+            for n in range(n0, n1):
+                finish(n)
+                if n + 3 < n1:
+                    head(n + 3)
+                if n + 4 == n1:
+                    prefill(u)
+                for job in jobs.get(n, ()):
+                    job()
+
+        def offsets(first, count, tag):
+            subtract_target(nc.gpsimd, first, tag)
+            for j in range(first + 1, first + count):
+                subtract_target(nc.gpsimd, j, "off%d" % j)
+
+        def widen_scale():
+            nc.scalar.copy(out=scale_col[:], in_=scale_in[:].rearrange("p g t -> p (g t)"))
+
+        prefill(0)
+        offsets(0, 4, "off0")
+        stage_one(0, 15, 18, None, {0: [iw(0, 0), iw(0, 1)], 1: [iw(0, 2)], 2: [iw(1, 0)], 3: [widen_scale, iw(1, 1)], 4: [iw(1, 2)], 5: [so(0)], 6: [so(1)]})
         quantize_h(0)
+        quantize_weight(0)
+        quantize_weight(1)
 
-        for u in range(UNITS - 1):
-            k = 3 * u
-            for j in range(2, 5):
-                subtract_target(nc.gpsimd, k + j)
-            head(2 * k)
-            if u > 0:
-                finish(2 * k - 2)
-            head(2 * k + 1)
-            if u > 0:
-                finish(2 * k - 1)
-                interleave_y(nc.scalar.copy, k - 1)
-            else:
-                scale_offset(0)
-            head(2 * k + 2)
-            scale_offset(k + 1)
-            for i in range(4):
-                step(4 * (u + 1) + i)
-                gather_turned(4 * (u + 1) + i)
-                if i == 1:
-                    scale_offset(k + 2)
-            for h in range(2 * k, 2 * k + 4):
-                finish(h)
-                if h < 2 * k + 3:
-                    head(h + 3)
-                if h == 2 * k + 1:
-                    interleave_y(nc.scalar.copy, k)
-                    scale_offset(k + 3)
-            interleave_y(nc.scalar.copy, k + 1)
-            if u > 0:
-                for c in range(3):
-                    quantize_y(k - 3 + c)
-                store_codes(u - 1, 0, C)
-            if u == 2:
-                store_scales(0)
-            quantize_h(u + 1)
+        offsets(4, 2, "w_in1")
+        stage_one(15, 19, 19, 0, {7: [so(2)], 8: [so(3)]}, (0, 1, 2))
+        drain(0, 4, 19, {3: [il(0, 0), il(0, 1)]})
+        quantize_h(1)
 
-        subtract_target(nc.gpsimd, 11)
-        scale_offset(10)
-        head(18)
-        finish(16)
-        head(19)
-        finish(17)
-        head(20)
-        interleave_y(nc.scalar.copy, 8)
-        scale_offset(11)
-        for h in range(18, 22):
-            finish(h)
-            if h < 21:
-                head(h + 3)
-            if h % 2 == 1:
-                interleave_y(nc.scalar.copy, h // 2)
-        for k in range(6, 9):
-            quantize_y(k)
-        store_codes(2, 0, C)
+        offsets(6, 3, "big1")
+        stage_one(19, 25, 25, 4, {9: [so(4)], 10: [so(5)], 11: [so(6)]}, (0, 4, 5))
+        drain(4, 10, 25, {7: [il(1, 0), il(1, 1), so(7)]})
+        quantize_y(0, 0, 512)
+        quantize_h(2)
+        store_codes(0, 0, 512)
+
+        offsets(9, 3, "big2")
+        stage_one(25, 32, 32, 10, {12: [so(8)], 13: [so(9)], 15: [so(10)]}, (0, 4, 5))
+        drain(10, 16, 32, {11: [il(2, 0), il(2, 1), so(11)], 15: [il(3, 0), il(3, 1)]})
+        quantize_h(3)
+        for n in range(16, 19):
+            head(n)
+        quantize_y(1, 0, 512)
+        quantize_y(2, 0, 512)
+        store_codes(0, 512, B * C)
+        store_scales(0)
+        for n in range(16, 22):
+            finish(n)
+            if n + 3 < 24:
+                head(n + 3)
+            if n == 19:
+                il(4, 0)()
+                il(4, 1)()
+        il(5, 0)()
+        quantize_y(3, 0, 512)
+        store_codes(1, 0, 512)
         finish(22)
         finish(23)
-        quantize_y(9)
-        interleave_y(nc.vector.tensor_copy, 11)
-        quantize_y(10)
-        store_codes(3, 0, 2 * CH)
-        quantize_y(11)
-        store_codes(3, 2 * CH, C)
+        quantize_y(4, 0, 512)
+        store_codes(1, 512, 1024)
+        interleave_y(nc.vector.tensor_copy, 6, 0, CH)
+        quantize_y(5, 0, CH)
+        quantize_y(6, 0, CH)
+        store_codes(1, 1024, B * C)
         store_scales(1)

@@ -40,6 +40,7 @@ def tile_soft_scatter_pixel_error_k5_kernel(
         e_raw = keep.tile([P, B * D // 2], I32)
         mask_rows = keep.tile([P, P], BF16)
         ident = keep.tile([P, P], F32)
+        sorter = keep.tile([P, P], F32)
         ident_bf = keep.tile([P, P], BF16)
         emb_in = keep.tile([P, D // P], BF16)
         bias_in = keep.tile([P, C // P], BF16)
@@ -77,18 +78,17 @@ def tile_soft_scatter_pixel_error_k5_kernel(
         nc.vector.memset(planes[:, 0:S_PLANE].bitcast(I32), 0)
         nc.vector.memset(planes[:, S_PLANE:].bitcast(I32), 0)
         nc.gpsimd.memset(mask_rows[:], 0.0)
-        nc.gpsimd.dma_start(out=emb_in[:], in_=mask_embedding.rearrange("(p j) -> p j", p=P))
         nc.gpsimd.dma_start(out=mask_rows[0 : L // P, :], in_=mask.rearrange("(i p) -> i p", p=P))
         make_identity(nc, ident[:])
         nc.gpsimd.dma_start(out=scale_in[:], in_=patch_scale.rearrange("(g p t) -> p g t", p=P, t=4))
-        load_scale_rows(nc.scalar, latent_scales, 0, S_PLANE)
+        load_scale_rows(nc.sync, latent_scales, 0, S_PLANE)
         nc.sync.dma_start(out=bias_in[:], in_=head_bias.rearrange("(p j) -> p j", p=P))
-        nc.sync.dma_start(out=s_words[:].bitcast(I32), in_=scatter_words[0].bitcast(I32))
+        nc.sync.dma_start(out=emb_in[:], in_=mask_embedding.rearrange("(p j) -> p j", p=P))
         nc.sync.dma_start(out=e_raw[:], in_=latent_words[0].bitcast(I32))
-        load_weight(0, 0)
-        nc.scalar.activation(out=ident_bf[:], in_=ident[:], func=ACT.Copy)
-        load_scale_rows(nc.scalar, scatter_scales, S_PLANE, L)
+        nc.sync.dma_start(out=s_words[:].bitcast(I32), in_=scatter_words[0].bitcast(I32))
+        load_scale_rows(nc.sync, scatter_scales, S_PLANE, L)
         load_target(0, 0, 2)
+        load_weight(0, 0)
         load_weight(0, 1)
         load_target(0, 2, 4)
         load_weight(1, 0)
@@ -102,6 +102,11 @@ def tile_soft_scatter_pixel_error_k5_kernel(
                 in_=source.rearrange("p (g q u x) -> p g u q x", u=2, q=16, x=run),
             )
 
+        nc.scalar.activation(out=ident_bf[:], in_=ident[:], func=ACT.Copy)
+        nc.scalar.copy(
+            out=sorter[:].rearrange("p (t j) -> p t j", t=4), in_=ident[:].rearrange("p (j t) -> p t j", t=4)
+        )
+
         def spread(bank, source, words):
             for w in range(words):
                 column = source[:].bitcast(F32)[:, w : w + 1]
@@ -112,15 +117,15 @@ def tile_soft_scatter_pixel_error_k5_kernel(
         spread(bias_bank, bias_in, 3)
         bias_words = bias_all[:].bitcast(F32).rearrange("p (q w) -> p q w", w=3)
         bias_turned = bias_bank[:, 0 : 3 * P].rearrange("p (w q) -> p q w", w=3)
-        nc.vector.tensor_copy(out=bias_words[:, 0:P, :], in_=bias_turned)
-        nc.vector.tensor_copy(out=bias_words[:, P : P + 43, :], in_=bias_turned[:, 0:43, :])
-        sort_columns(e_words[:].bitcast(I32), e_raw[:], 8)
+        nc.scalar.copy(out=bias_words[:, 0:P, :], in_=bias_turned)
+        nc.scalar.copy(out=bias_words[:, P : P + 43, :], in_=bias_turned[:, 0:43, :])
         emb_bank = psum.tile([P, 512], F32, tag="h0")
         spread(emb_bank, emb_in, 4)
         nc.vector.tensor_copy(
             out=emb_all[:].bitcast(F32).rearrange("p (u q h w) -> p u q h w", u=2, h=2, w=4),
             in_=emb_bank[:].rearrange("p (w q u h) -> p u q h w", w=4, u=2, h=2),
         )
+        sort_columns(e_words[:].bitcast(I32), e_raw[:], 8)
         mask_bank = psum.tile([P, P], BF16, tag="h1")
         nc.tensor.transpose(mask_bank[:], mask_rows[:], ident_bf[:])
         nc.vector.tensor_copy(out=mask_col[:], in_=mask_bank[:, 0 : L // P])
@@ -188,7 +193,7 @@ def tile_soft_scatter_pixel_error_k5_kernel(
             bank = stage_one_bank()
             words = h_rows[step][:].bitcast(F32)
             for k in range(4):
-                nc.tensor.transpose(bank[:, P * k : P * (k + 1)], words[:, P * k : P * (k + 1)], ident[:])
+                nc.tensor.transpose(bank[:, P * k : P * (k + 1)], words[:, P * k : P * (k + 1)], sorter[:])
             turned[step] = bank
 
         def gather_turned(step):
@@ -198,7 +203,7 @@ def tile_soft_scatter_pixel_error_k5_kernel(
             words = h_in[u][:].bitcast(F32).rearrange("p (g t i j u) -> p g t i j u", g=2, t=4, i=4, u=2)
             nc.scalar.copy(
                 out=words[:, :, :, i],
-                in_=turned[step][:].rearrange("p (g u j t) -> p g t j u", g=2, u=2, t=4),
+                in_=turned[step][:].rearrange("p (g u t j) -> p g t j u", g=2, u=2, t=4),
             )
 
         def quantize_h(u):
@@ -288,8 +293,8 @@ def tile_soft_scatter_pixel_error_k5_kernel(
                 tag = "y_in%d" % k
                 y_in[k] = keep.tile([P, PIECES[k][2], 4], BF16, tag=tag, align_bytes=64, name="y_in")
             copy(
-                out=y_in[k][:, a:b, :].rearrange("p (c i) t -> p c t i", i=4),
-                in_=ys[k][:, :, a:b].rearrange("p t (c i) -> p c t i", i=4),
+                out=y_in[k][:, a:b, :].rearrange("p (c i) t -> p c t i", i=2),
+                in_=ys[k][:, :, a:b].rearrange("p t (c i) -> p c t i", i=2),
             )
 
         def quantize_y(k, a, b):

@@ -17,10 +17,26 @@ ALU = mybir.AluOpType
 ACT = mybir.ActivationFunctionType
 
 P = 128
-GROUP = 512
-CH = 256
-UNITS = 4
+SLOTS = 4
+GROUP = P * SLOTS
+BANK = 512
+CHUNK = 256
+RUN = 4
+
+PASSES = 32
+AHEAD = 3
+STAGE_ONE_BANKS = 5
+
 PIECES = [(0, 0, 512), (0, 512, 512), (0, 1024, 512), (1, 0, 512), (1, 512, 512), (1, 1024, 256), (1, 1280, 256)]
+WIDE = 5
+RESULT_BANKS = 24
+BIAS_WRAP = 43
+
+PASS_ENDS = (14, 18, 25, PASSES)
+BANK_ENDS = (0, 4, 10, 16)
+PART_ENDS = (4, 6, 9, 12)
+SCALE_LAG = 5
+
 S_PLANE = B * D
 
 
@@ -44,57 +60,64 @@ def tile_soft_scatter_pixel_error_k5_kernel(
         ident_bf = keep.tile([P, P], BF16)
         emb_in = keep.tile([P, D // P], BF16)
         bias_in = keep.tile([P, C // P], BF16)
-        scale_in = keep.tile([P, 2, 4], BF16)
+        scale_in = keep.tile([P, 2, SLOTS], BF16)
         s_words = keep.tile([P, 2 * L], U8, align_bytes=64)
         e_words = keep.tile([P, 2 * B * D], U8, align_bytes=64)
-        w_raw = [keep.tile([P, 4, C], BF16, name="w_raw%d" % g) for g in range(2)]
-        w_in = [keep.tile([P, C, 4], BF16, align_bytes=64, tag="w_in%d" % g, name="w_in") for g in range(2)]
+        w_raw = [keep.tile([P, SLOTS, C], BF16, name="w_raw%d" % g) for g in range(2)]
+        w_in = [keep.tile([P, C, SLOTS], BF16, align_bytes=64, tag="w_in%d" % g, name="w_in") for g in range(2)]
         w_codes = [keep.tile([P, C], U32, align_bytes=64, name="w_codes%d" % g) for g in range(2)]
         w_scales = [keep.tile([P, C], U8, align_bytes=64, name="w_scales%d" % g) for g in range(2)]
-        tgt = [keep.tile([P, 4, w], BF16, name="tgt%d" % k) for k, (g, c0, w) in enumerate(PIECES)]
+        tgt = [keep.tile([P, SLOTS, width], BF16, name="tgt%d" % k) for k, (g, c0, width) in enumerate(PIECES)]
         emb_all = keep.tile([P, D], BF16)
-        bias_all = keep.tile([P, C + 6 * 43], BF16)
+        bias_all = keep.tile([P, C + 6 * BIAS_WRAP], BF16)
         mask_col = keep.tile([P, L // P], F32)
-        scale_col = keep.tile([P, 8], F32)
+        scale_col = keep.tile([P, 2 * SLOTS], F32)
         y_codes = [keep.tile([P, B * C], U32, align_bytes=64, name="y_codes%d" % g) for g in range(2)]
         y_scales = [keep.tile([P, B * C], U8, align_bytes=64, name="y_scales%d" % g) for g in range(2)]
 
-        def load_scale_rows(engine, source, col0, width):
-            for q in range(4):
-                engine.dma_start(
-                    out=planes[32 * q : 32 * q + 4, col0 : col0 + width].bitcast(I32),
-                    in_=source[0, 4 * q : 4 * q + 4, :].bitcast(I32),
+
+        def load_scale_rows(source, col0, width):
+            for quadrant in range(4):
+                nc.sync.dma_start(
+                    out=planes[32 * quadrant : 32 * quadrant + 4, col0 : col0 + width].bitcast(I32),
+                    in_=source[0, 4 * quadrant : 4 * quadrant + 4, :].bitcast(I32),
                 )
 
         def load_weight(g, u):
             rows = head_weight[GROUP * g : GROUP * (g + 1), :].rearrange("(q u r e) c -> u q r (e c)", u=2, r=8, e=2)
             nc.sync.dma_start(out=w_raw[g][:, 2 * u : 2 * u + 2, :].rearrange("p e c -> p (e c)"), in_=rows[u])
 
-        def load_target(k, t0=0, t1=4):
-            g, c0, w = PIECES[k]
-            rows = target[GROUP * g : GROUP * (g + 1)].rearrange("(p t) r c -> p t (r c)", t=4)
-            nc.sync.dma_start(out=tgt[k][:, t0:t1, :], in_=rows[:, t0:t1, c0 : c0 + w])
+        def load_target(k, t0=0, t1=SLOTS):
+            g, c0, width = PIECES[k]
+            rows = target[GROUP * g : GROUP * (g + 1)].rearrange("(p t) r c -> p t (r c)", t=SLOTS)
+            nc.sync.dma_start(out=tgt[k][:, t0:t1, :], in_=rows[:, t0:t1, c0 : c0 + width])
 
         nc.vector.memset(planes[:, 0:S_PLANE].bitcast(I32), 0)
+        nc.vector.memset(mask_rows[:], 0.0)
         nc.vector.memset(planes[:, S_PLANE:].bitcast(I32), 0)
-        nc.gpsimd.memset(mask_rows[:], 0.0)
-        nc.gpsimd.dma_start(out=mask_rows[0 : L // P, :], in_=mask.rearrange("(i p) -> i p", p=P))
         make_identity(nc, ident[:])
-        nc.gpsimd.dma_start(out=scale_in[:], in_=patch_scale.rearrange("(g p t) -> p g t", p=P, t=4))
-        load_scale_rows(nc.sync, latent_scales, 0, S_PLANE)
+        by_slot = ident[:].rearrange("p (j t) -> p t j", t=SLOTS)
+        nc.gpsimd.tensor_tensor(
+            out=sorter[:].rearrange("p (t j) -> p t j", t=SLOTS), in0=by_slot, in1=by_slot, op=ALU.mult
+        )
+        load_scale_rows(latent_scales, 0, S_PLANE)
         nc.sync.dma_start(out=bias_in[:], in_=head_bias.rearrange("(p j) -> p j", p=P))
         nc.sync.dma_start(out=emb_in[:], in_=mask_embedding.rearrange("(p j) -> p j", p=P))
+        nc.sync.dma_start(out=mask_rows[0 : L // P, :], in_=mask.rearrange("(i p) -> i p", p=P))
         nc.sync.dma_start(out=e_raw[:], in_=latent_words[0].bitcast(I32))
-        nc.sync.dma_start(out=s_words[:].bitcast(I32), in_=scatter_words[0].bitcast(I32))
-        load_scale_rows(nc.sync, scatter_scales, S_PLANE, L)
+        load_scale_rows(scatter_scales, S_PLANE, L)
         load_target(0, 0, 2)
+        nc.sync.dma_start(out=s_words[:].bitcast(I32), in_=scatter_words[0].bitcast(I32))
         load_weight(0, 0)
         load_weight(0, 1)
-        load_target(0, 2, 4)
+        load_target(0, 2, SLOTS)
+        load_target(1)
         load_weight(1, 0)
         load_weight(1, 1)
-        for k in range(1, len(PIECES)):
+        nc.sync.dma_start(out=scale_in[:], in_=patch_scale.rearrange("(g p t) -> p g t", p=P, t=SLOTS))
+        for k in range(2, len(PIECES)):
             load_target(k)
+
 
         def sort_columns(out, source, run):
             nc.vector.tensor_copy(
@@ -102,42 +125,38 @@ def tile_soft_scatter_pixel_error_k5_kernel(
                 in_=source.rearrange("p (g q u x) -> p g u q x", u=2, q=16, x=run),
             )
 
-        nc.scalar.activation(out=ident_bf[:], in_=ident[:], func=ACT.Copy)
-        nc.scalar.copy(
-            out=sorter[:].rearrange("p (t j) -> p t j", t=4), in_=ident[:].rearrange("p (j t) -> p t j", t=4)
-        )
-
         def spread(bank, source, words):
             for w in range(words):
                 column = source[:].bitcast(F32)[:, w : w + 1]
                 nc.tensor.transpose(bank[:, P * w : P * (w + 1)], column.to_broadcast([P, P]), ident[:])
 
+        nc.scalar.activation(out=ident_bf[:], in_=ident[:], func=ACT.Copy)
         sort_columns(e_scales[:].bitcast(I32), planes[:, 0:S_PLANE].bitcast(I32), 4)
-        bias_bank = psum.tile([P, 512], F32, tag="h2")
+        bias_bank = psum.tile([P, BANK], F32, tag="two2")
         spread(bias_bank, bias_in, 3)
         bias_words = bias_all[:].bitcast(F32).rearrange("p (q w) -> p q w", w=3)
         bias_turned = bias_bank[:, 0 : 3 * P].rearrange("p (w q) -> p q w", w=3)
         nc.scalar.copy(out=bias_words[:, 0:P, :], in_=bias_turned)
-        nc.scalar.copy(out=bias_words[:, P : P + 43, :], in_=bias_turned[:, 0:43, :])
-        emb_bank = psum.tile([P, 512], F32, tag="h0")
+        nc.scalar.copy(out=bias_words[:, P : P + BIAS_WRAP, :], in_=bias_turned[:, 0:BIAS_WRAP, :])
+        emb_bank = psum.tile([P, BANK], F32, tag="two0")
         spread(emb_bank, emb_in, 4)
-        nc.vector.tensor_copy(
-            out=emb_all[:].bitcast(F32).rearrange("p (u q h w) -> p u q h w", u=2, h=2, w=4),
-            in_=emb_bank[:].rearrange("p (w q u h) -> p u q h w", w=4, u=2, h=2),
+        nc.scalar.copy(
+            out=emb_all[:].bitcast(F32).rearrange("p (u b h w) -> p u b h w", u=2, h=2, w=4),
+            in_=emb_bank[:].rearrange("p (w b u h) -> p u b h w", w=4, u=2, h=2),
         )
-        sort_columns(e_words[:].bitcast(I32), e_raw[:], 8)
-        mask_bank = psum.tile([P, P], BF16, tag="h1")
+        for r in range(B):
+            image = slice(D // 2 * r, D // 2 * (r + 1))
+            sort_columns(e_words[:].bitcast(I32)[:, image], e_raw[:, image], 8)
+        mask_bank = psum.tile([P, P], BF16, tag="two1")
         nc.tensor.transpose(mask_bank[:], mask_rows[:], ident_bf[:])
-        nc.vector.tensor_copy(out=mask_col[:], in_=mask_bank[:, 0 : L // P])
+        nc.scalar.copy(out=mask_col[:], in_=mask_bank[:, 0 : L // P])
 
-        mix_banks, head_banks, h_rows, h_in, h_codes, h_scales = {}, {}, {}, {}, {}, {}
-        offs, ys, y_in = {}, {}, {}
 
-        def interleave_weight(copy, g, c):
-            cols = slice(CH * c, CH * (c + 1))
-            copy(
-                out=w_in[g][:, cols, :].rearrange("p (c i) j -> p c j i", i=4),
-                in_=w_raw[g][:, :, cols].rearrange("p j (c i) -> p c j i", i=4),
+        def interleave_weight(g, chunk):
+            cols = slice(CHUNK * chunk, CHUNK * (chunk + 1))
+            nc.scalar.copy(
+                out=w_in[g][:, cols, :].rearrange("p (c i) t -> p c t i", i=RUN),
+                in_=w_raw[g][:, :, cols].rearrange("p t (c i) -> p c t i", i=RUN),
             )
 
         def quantize_weight(g):
@@ -145,24 +164,24 @@ def tile_soft_scatter_pixel_error_k5_kernel(
                 nc.vector.quantize_mx(
                     out=w_codes[g][:, c0:c1].bitcast(FP8X4),
                     scales=w_scales[g][:, c0:c1],
-                    in_=w_in[g][:, c0:c1, :].rearrange("p c j -> p (c j)"),
+                    in_=w_in[g][:, c0:c1, :].rearrange("p c t -> p (c t)"),
                 )
 
-        taken = []
+
+        taken, mixed, h_rows, h_in, h_codes, h_scales = [], {}, {}, {}, {}, {}
 
         def stage_one_bank():
-            taken.append(psum.tile([P, 512], F32, tag="a%d" % (len(taken) % 5), name="stage_one_bank"))
+            tag = "one%d" % (len(taken) % STAGE_ONE_BANKS)
+            taken.append(psum.tile([P, BANK], F32, tag=tag, name="stage_one_bank"))
             return taken[-1]
 
         def mix(m):
-            if m >= 8 * UNITS:
-                return
-            u, i, g = m // 8, m % 8 // 2, m % 2
-            l0 = GROUP * (u // 2) + P * i
-            d0 = D * (u % 2) + GROUP * g
-            bank = stage_one_bank()
+            unit, g = m // 8, m % 2
+            l0 = GROUP * (unit // 2) + P * (m // 2 % 4)
+            d0 = D * (unit % 2) + GROUP * g
+            mixed[m] = stage_one_bank()
             nc.tensor.matmul_mx(
-                out=bank[:],
+                out=mixed[m][:],
                 lhsT=s_words[:, 2 * l0 : 2 * (l0 + P)].bitcast(FP4X4),
                 lhsT_scale=planes[:, S_PLANE + l0 : S_PLANE + l0 + P],
                 rhs=e_words[:, 2 * d0 : 2 * (d0 + GROUP)].bitcast(FP4X4),
@@ -170,242 +189,232 @@ def tile_soft_scatter_pixel_error_k5_kernel(
                 start=True,
                 stop=True,
             )
-            mix_banks[m] = bank
 
         def add_embedding(m):
-            u, i, g = m // 8, m % 8 // 2, m % 2
+            step, g = m // 2, m % 2
             if g == 0:
-                h_rows[m // 2] = ring.tile([P, D], BF16, tag="h_rows", bufs=4, name="h_rows")
-            tile_col = 4 * (u // 2) + i
-            cols = slice(GROUP * g, GROUP * (g + 1))
+                h_rows[step] = ring.tile([P, D], BF16, tag="h_rows", bufs=4, name="h_rows")
+            i = 4 * (m // 16) + step % 4
             nc.vector.scalar_tensor_tensor(
-                out=h_rows[m // 2][:, cols].rearrange("p (u x) -> p u x", u=2),
+                out=h_rows[step][:, GROUP * g : GROUP * (g + 1)].rearrange("p (u x) -> p u x", u=2),
                 in0=emb_all[:].rearrange("p (u g x) -> p u g x", u=2, g=2)[:, :, g, :],
-                scalar=mask_col[:, tile_col : tile_col + 1],
-                in1=mix_banks[m][:].rearrange("p (u x) -> p u x", u=2),
+                scalar=mask_col[:, i : i + 1],
+                in1=mixed[m][:].rearrange("p (u x) -> p u x", u=2),
                 op0=ALU.mult,
                 op1=ALU.add,
             )
 
-        turned = {}
-
         def turn(step):
+            unit = step // 4
             bank = stage_one_bank()
-            words = h_rows[step][:].bitcast(F32)
-            for k in range(4):
-                nc.tensor.transpose(bank[:, P * k : P * (k + 1)], words[:, P * k : P * (k + 1)], sorter[:])
-            turned[step] = bank
-
-        def gather_turned(step):
-            u, i = step // 4, step % 4
-            if i == 0:
-                h_in[u] = keep.tile([P, 4096], BF16, tag="big%d" % u, align_bytes=64, name="h_in")
-            words = h_in[u][:].bitcast(F32).rearrange("p (g t i j u) -> p g t i j u", g=2, t=4, i=4, u=2)
+            rows = h_rows[step][:].bitcast(F32)
+            for quarter in range(4):
+                cols = slice(P * quarter, P * (quarter + 1))
+                nc.tensor.transpose(bank[:, cols], rows[:, cols], sorter[:])
+            if step % 4 == 0:
+                h_in[unit] = keep.tile([P, 2 * GROUP * SLOTS], BF16, tag="h_in%d" % unit, align_bytes=64, name="h_in")
+            laid = h_in[unit][:].bitcast(F32).rearrange("p (g t i j u) -> p g t i j u", g=2, t=SLOTS, i=4, u=2)
             nc.scalar.copy(
-                out=words[:, :, :, i],
-                in_=turned[step][:].rearrange("p (g u t j) -> p g t j u", g=2, u=2, t=4),
+                out=laid[:, :, :, step % 4],
+                in_=bank[:].rearrange("p (g u t j) -> p g t j u", g=2, u=2, t=SLOTS),
             )
 
-        def quantize_h(u):
-            h_codes[u] = ring.tile([P, 2 * GROUP], U32, tag="h_codes", align_bytes=64, name="h_codes")
-            h_scales[u] = ring.tile([P, 2 * GROUP], U8, tag="h_scales", align_bytes=64, name="h_scales")
-            nc.vector.quantize_mx(out=h_codes[u][:].bitcast(FP8X4), scales=h_scales[u][:], in_=h_in[u][:])
+        def quantize_h(unit):
+            h_codes[unit] = ring.tile([P, 2 * GROUP], U32, tag="h_codes", align_bytes=64, name="h_codes")
+            h_scales[unit] = ring.tile([P, 2 * GROUP], U8, tag="h_scales", align_bytes=64, name="h_scales")
+            nc.vector.quantize_mx(out=h_codes[unit][:].bitcast(FP8X4), scales=h_scales[unit][:], in_=h_in[unit][:])
+
+
+        offsets, summed, ys, y_in = {}, {}, {}, {}
 
         def place(j):
-            k = j // 2 if j < 10 else j - 5
-            slots = range(2 * (j % 2), 2 * (j % 2) + 2) if j < 10 else range(4)
-            return k, slots
+            if j < 2 * WIDE:
+                return j // 2, range(2 * (j % 2), 2 * (j % 2) + 2)
+            return j - WIDE, range(SLOTS)
 
         def subtract_target(engine, j, tag):
             k, slots = place(j)
-            g, c0, w = PIECES[k]
-            offs[j] = keep.tile([P, len(slots), w], F32, tag=tag, align_bytes=64, name="off")
+            g, c0, width = PIECES[k]
+            offsets[j] = keep.tile([P, len(slots), width], F32, tag=tag, align_bytes=64, name="offset")
+            bias = bias_all[:, c0 % C : c0 % C + width].rearrange("p (o c) -> p o c", o=1)
             engine.tensor_tensor(
-                out=offs[j][:],
-                in0=bias_all[:, c0 % C : c0 % C + w].rearrange("p (o c) -> p o c", o=1).to_broadcast([P, len(slots), w]),
+                out=offsets[j][:],
+                in0=bias.to_broadcast([P, len(slots), width]),
                 in1=tgt[k][:, slots.start : slots.stop, :],
                 op=ALU.subtract,
             )
 
+        def patch_scales(g, t):
+            return scale_col[:, SLOTS * g + t : SLOTS * g + t + 1]
+
         def scale_offset(j):
             k, slots = place(j)
-            g = PIECES[k][0]
-            for s, t in enumerate(slots):
-                nc.scalar.activation(
-                    out=offs[j][:, s, :], in_=offs[j][:, s, :], func=ACT.Copy,
-                    scale=scale_col[:, 4 * g + t : 4 * g + t + 1],
-                )
+            for row, t in enumerate(slots):
+                values = offsets[j][:, row, :]
+                nc.scalar.activation(out=values, in_=values, func=ACT.Copy, scale=patch_scales(PIECES[k][0], t))
 
-        def bank_slots(n):
+        def bank_rows(n):
             k, slots = place(n // 2)
             each = len(slots) // 2
-            return k, range(each * (n % 2), each * (n % 2 + 1)), slots
+            return k, slots, range(each * (n % 2), each * (n % 2 + 1))
 
-        def head(n):
-            k, local, slots = bank_slots(n)
-            g, c0, w = PIECES[k]
-            bank = psum.tile([P, 512], F32, tag="h%d" % (n % 3), name="head_bank")
-            at = 0
-            for s in local:
-                t = slots[s]
-                cuts = [c0, C, c0 + w] if c0 < C < c0 + w else [c0, c0 + w]
+        def predict(n):
+            k, slots, rows = bank_rows(n)
+            g, c0, width = PIECES[k]
+            summed[n] = psum.tile([P, BANK], F32, tag="two%d" % (n % AHEAD), name="result_bank")
+            cuts = [c0, C, c0 + width] if c0 < C < c0 + width else [c0, c0 + width]
+            for at, row in enumerate(rows):
                 for a, b in zip(cuts, cuts[1:]):
-                    u = 2 * g + a // C
-                    cols = slice(a % C, a % C + b - a)
+                    unit = 2 * g + a // C
+                    pixels = slice(a % C, a % C + b - a)
                     for half in range(2):
-                        rows = slice(GROUP * half + P * t, GROUP * half + P * (t + 1))
+                        first = GROUP * half + P * slots[row]
                         nc.tensor.matmul_mx(
-                            out=bank[:, at : at + b - a],
-                            lhsT=h_codes[u][:, rows].bitcast(FP8X4),
-                            lhsT_scale=h_scales[u][:, rows],
-                            rhs=w_codes[half][:, cols].bitcast(FP8X4),
-                            rhs_scale=w_scales[half][:, cols],
+                            out=summed[n][:, width * at + a - c0 : width * at + b - c0],
+                            lhsT=h_codes[unit][:, first : first + P].bitcast(FP8X4),
+                            lhsT_scale=h_scales[unit][:, first : first + P],
+                            rhs=w_codes[half][:, pixels].bitcast(FP8X4),
+                            rhs_scale=w_scales[half][:, pixels],
                             start=(half == 0),
                             stop=(half == 1),
                         )
-                    at += b - a
-            head_banks[n] = bank
 
         def finish(n):
-            j = n // 2
-            k, local, slots = bank_slots(n)
-            g, c0, w = PIECES[k]
+            k, slots, rows = bank_rows(n)
+            g, c0, width = PIECES[k]
             if k not in ys:
-                ys[k] = ring.tile([P, 4, w], F32, tag="y", bufs=4, name="y")
-            for at, s in enumerate(local):
-                t = slots[s]
+                ys[k] = ring.tile([P, SLOTS, width], F32, tag="y", bufs=4, name="y")
+            for at, row in enumerate(rows):
                 nc.vector.scalar_tensor_tensor(
-                    out=ys[k][:, t, :],
-                    in0=head_banks[n][:, w * at : w * (at + 1)],
-                    scalar=scale_col[:, 4 * g + t : 4 * g + t + 1],
-                    in1=offs[j][:, s, :],
+                    out=ys[k][:, slots[row], :],
+                    in0=summed[n][:, width * at : width * (at + 1)],
+                    scalar=patch_scales(g, slots[row]),
+                    in1=offsets[n // 2][:, row, :],
                     op0=ALU.mult,
                     op1=ALU.add,
                 )
             if n % 2 == 1:
-                rows = out_0[GROUP * g : GROUP * (g + 1)].rearrange("(p t) r c -> p t (r c)", t=4)
+                stored = out_0[GROUP * g : GROUP * (g + 1)].rearrange("(p t) r c -> p t (r c)", t=SLOTS)
                 nc.sync.dma_start(
-                    out=rows[:, slots.start : slots.stop, c0 : c0 + w], in_=ys[k][:, slots.start : slots.stop, :]
+                    out=stored[:, slots.start : slots.stop, c0 : c0 + width],
+                    in_=ys[k][:, slots.start : slots.stop, :],
                 )
 
-        def interleave_y(copy, k, a, b):
-            if k not in y_in:
-                tag = "y_in%d" % k
-                y_in[k] = keep.tile([P, PIECES[k][2], 4], BF16, tag=tag, align_bytes=64, name="y_in")
-            copy(
-                out=y_in[k][:, a:b, :].rearrange("p (c i) t -> p c t i", i=2),
-                in_=ys[k][:, :, a:b].rearrange("p t (c i) -> p c t i", i=2),
-            )
+        def interleave_y(copy, k):
+            width = PIECES[k][2]
+            y_in[k] = keep.tile([P, width, SLOTS], BF16, tag="y_in%d" % k, align_bytes=64, name="y_in")
+            for c0 in range(0, width, CHUNK):
+                copy(
+                    out=y_in[k][:, c0 : c0 + CHUNK, :].rearrange("p (c i) t -> p c t i", i=RUN),
+                    in_=ys[k][:, :, c0 : c0 + CHUNK].rearrange("p t (c i) -> p c t i", i=RUN),
+                )
 
-        def quantize_y(k, a, b):
-            g, c0, w = PIECES[k]
+        def quantize_y(k):
+            g, c0, width = PIECES[k]
             nc.vector.quantize_mx(
-                out=y_codes[g][:, c0 + a : c0 + b].bitcast(FP8X4),
-                scales=y_scales[g][:, c0 + a : c0 + b],
-                in_=y_in[k][:, a:b, :].rearrange("p c t -> p (c t)"),
+                out=y_codes[g][:, c0 : c0 + width].bitcast(FP8X4),
+                scales=y_scales[g][:, c0 : c0 + width],
+                in_=y_in[k][:].rearrange("p c t -> p (c t)"),
             )
 
-        def store_codes(g, a, b):
-            words = out_1[g].rearrange("p n t -> p (n t)")
-            nc.sync.dma_start(out=words[:, 4 * a : 4 * b].bitcast(I32), in_=y_codes[g][:, a:b].bitcast(I32))
+        def store_codes(k0, k1):
+            g, a, b = PIECES[k0][0], PIECES[k0][1], PIECES[k1][1] + PIECES[k1][2]
+            stored = out_1[g].rearrange("p n t -> p (n t)")
+            nc.sync.dma_start(out=stored[:, SLOTS * a : SLOTS * b].bitcast(I32), in_=y_codes[g][:, a:b].bitcast(I32))
 
         def store_scales(g):
-            for q in range(4):
-                engine = nc.scalar if g == 1 and q % 2 else nc.sync
-                engine.dma_start(
-                    out=out_2[g, 4 * q : 4 * q + 4, :].bitcast(I32),
-                    in_=y_scales[g][32 * q : 32 * q + 4, :].bitcast(I32),
+            for quadrant in range(4):
+                nc.sync.dma_start(
+                    out=out_2[g, 4 * quadrant : 4 * quadrant + 4, :].bitcast(I32),
+                    in_=y_scales[g][32 * quadrant : 32 * quadrant + 4, :].bitcast(I32),
                 )
 
-        def il(k, half):
-            return lambda: interleave_y(nc.scalar.copy, k, CH * half, CH * (half + 1))
 
-        def so(j):
-            return lambda: scale_offset(j)
+        def ahead_of_turn(step):
+            if step < 6:
+                interleave_weight(step // 3, step % 3)
+            if step == SCALE_LAG:
+                nc.scalar.copy(out=scale_col[:], in_=scale_in[:].rearrange("p g t -> p (g t)"))
+            if step >= SCALE_LAG:
+                scale_offset(step - SCALE_LAG)
 
-        def iw(g, c):
-            return lambda: interleave_weight(nc.scalar.copy, g, c)
+        def behind_bank(n):
+            if n % 4 == 3 and n // 4 < WIDE:
+                interleave_y(nc.scalar.copy, n // 4)
+                if BANK_ENDS[-2] <= n < BANK_ENDS[-1] - 1:
+                    scale_offset(PART_ENDS[-1] - 1)
 
-        def stage_one(first, last, ahead_to, n0, jobs, head_at=()):
-            for m in range(first, last):
-                if n0 is not None and m - first in head_at:
-                    head(n0 + head_at.index(m - first))
+        def window(w, held):
+            pass0, pass1 = PASS_ENDS[w - 1], PASS_ENDS[w]
+            bank0, bank1 = BANK_ENDS[w - 1], BANK_ENDS[w]
+            for j in range(PART_ENDS[w - 1], PART_ENDS[w]):
+                subtract_target(nc.gpsimd, j, held if j == PART_ENDS[w - 1] else "offset%d" % j)
+            fills = (pass0, pass1 - 3, pass1 - 2)
+            for m in range(pass0, pass1):
+                if m in fills:
+                    predict(bank0 + fills.index(m))
                 add_embedding(m)
-                if m + 3 < ahead_to:
-                    mix(m + 3)
-                if m % 2:
-                    for job in jobs.get(m // 2, ()):
-                        job()
+                if m + AHEAD < pass1:
+                    mix(m + AHEAD)
+                if m % 2 == 1:
+                    ahead_of_turn(m // 2)
                     turn(m // 2)
-                    gather_turned(m // 2)
-
-        def prefill(first):
-            for m in range(first, first + 3):
-                mix(m)
-
-        def drain(n0, n1, u, jobs):
-            for n in range(n0, n1):
+            for n in range(bank0, bank1):
                 finish(n)
-                if n + 3 < n1:
-                    head(n + 3)
-                if n + 4 == n1:
-                    prefill(u)
-                for job in jobs.get(n, ()):
-                    job()
+                if n + AHEAD < bank1:
+                    predict(n + AHEAD)
+                if n + AHEAD + 1 == bank1:
+                    for m in range(pass1, min(pass1 + AHEAD, PASSES)):
+                        mix(m)
+                behind_bank(n)
 
-        def offsets(first, count, tag):
-            subtract_target(nc.gpsimd, first, tag)
-            for j in range(first + 1, first + count):
-                subtract_target(nc.gpsimd, j, "off%d" % j)
-
-        def widen_scale():
-            nc.scalar.copy(out=scale_col[:], in_=scale_in[:].rearrange("p g t -> p (g t)"))
-
-        prefill(0)
-        offsets(0, 4, "off0")
-        stage_one(0, 15, 18, None, {0: [iw(0, 0), iw(0, 1)], 1: [iw(0, 2)], 2: [iw(1, 0)], 3: [widen_scale, iw(1, 1)], 4: [iw(1, 2)], 5: [so(0)], 6: [so(1)]})
+        for m in range(AHEAD):
+            mix(m)
+        subtract_target(nc.vector, 0, "offset0")
+        for j in range(1, PART_ENDS[0]):
+            subtract_target(nc.gpsimd, j, "offset%d" % j)
+        for m in range(PASS_ENDS[0]):
+            add_embedding(m)
+            mix(m + AHEAD)
+            if m % 2 == 1:
+                ahead_of_turn(m // 2)
+                turn(m // 2)
         quantize_h(0)
         quantize_weight(0)
         quantize_weight(1)
 
-        offsets(4, 2, "w_in1")
-        stage_one(15, 19, 19, 0, {7: [so(2)], 8: [so(3)]}, (0, 1, 2))
-        drain(0, 4, 19, {3: [il(0, 0), il(0, 1)]})
+        window(1, "w_in1")
         quantize_h(1)
 
-        offsets(6, 3, "big1")
-        stage_one(19, 25, 25, 4, {9: [so(4)], 10: [so(5)], 11: [so(6)]}, (0, 4, 5))
-        drain(4, 10, 25, {7: [il(1, 0), il(1, 1), so(7)]})
-        quantize_y(0, 0, 512)
+        window(2, "h_in1")
+        quantize_y(0)
         quantize_h(2)
-        store_codes(0, 0, 512)
+        store_codes(0, 0)
 
-        offsets(9, 3, "big2")
-        stage_one(25, 32, 32, 10, {12: [so(8)], 13: [so(9)], 15: [so(10)]}, (0, 4, 5))
-        drain(10, 16, 32, {11: [il(2, 0), il(2, 1), so(11)], 15: [il(3, 0), il(3, 1)]})
+        window(3, "h_in2")
         quantize_h(3)
-        for n in range(16, 19):
-            head(n)
-        quantize_y(1, 0, 512)
-        quantize_y(2, 0, 512)
-        store_codes(0, 512, B * C)
+
+        first, last_piece = BANK_ENDS[-1], len(PIECES) - 1
+        for n in range(first, first + AHEAD):
+            predict(n)
+        quantize_y(1)
+        quantize_y(2)
+        store_codes(1, 2)
         store_scales(0)
-        for n in range(16, 22):
+        for n in range(first, RESULT_BANKS - 2):
             finish(n)
-            if n + 3 < 24:
-                head(n + 3)
-            if n == 19:
-                il(4, 0)()
-                il(4, 1)()
-        il(5, 0)()
-        quantize_y(3, 0, 512)
-        store_codes(1, 0, 512)
-        finish(22)
-        finish(23)
-        quantize_y(4, 0, 512)
-        store_codes(1, 512, 1024)
-        interleave_y(nc.vector.tensor_copy, 6, 0, CH)
-        quantize_y(5, 0, CH)
-        quantize_y(6, 0, CH)
-        store_codes(1, 1024, B * C)
+            if n + AHEAD < RESULT_BANKS:
+                predict(n + AHEAD)
+            behind_bank(n)
+        interleave_y(nc.scalar.copy, last_piece - 1)
+        quantize_y(3)
+        store_codes(3, 3)
+        finish(RESULT_BANKS - 2)
+        finish(RESULT_BANKS - 1)
+        quantize_y(4)
+        interleave_y(nc.vector.tensor_copy, last_piece)
+        quantize_y(last_piece - 1)
+        store_codes(4, last_piece - 1)
+        quantize_y(last_piece)
+        store_codes(last_piece, last_piece)
         store_scales(1)

from contextlib import ExitStack

import concourse.mybir as mybir
from concourse.masks import make_identity

L, V, B, D, C = 1024, 512, 2, 1024, 768
FLOPS = 2 * V * L * B * D + 2 * L * B * D * C

F32 = mybir.dt.float32
BF16 = mybir.dt.bfloat16
I32 = mybir.dt.int32
U32 = mybir.dt.uint32
U8 = mybir.dt.uint8
FP8X4 = mybir.dt.float8_e4m3fn_x4
FP4X4 = mybir.dt.float4_e2m1fn_x4
ALU = mybir.AluOpType
ACT = mybir.ActivationFunctionType

P = 128
SLOTS = 4
GROUP = P * SLOTS
BANK = 512
CHUNK = 256
RUN = 4

PASSES = 32
AHEAD = 3
STAGE_ONE_BANKS = 5

PIECES = [(0, 0, 512), (0, 512, 512), (0, 1024, 512), (1, 0, 512), (1, 512, 512), (1, 1024, 256), (1, 1280, 256)]
WIDE = 5
RESULT_BANKS = 24
BIAS_WRAP = 43

PASS_ENDS = (14, 18, 25, PASSES)
BANK_ENDS = (0, 4, 10, 16)
PART_ENDS = (4, 6, 9, 12)
SCALE_LAG = 5

S_PLANE = B * D


def tile_soft_scatter_pixel_error_k5_kernel(
    tc, scatter_words, scatter_scales, latent_words, latent_scales, mask, mask_embedding,
    head_weight, head_bias, target, patch_scale, out_0, out_1, out_2,
):
    nc = tc.nc
    with ExitStack() as ctx:
        keep = ctx.enter_context(tc.tile_pool(name="keep", bufs=1))
        ring = ctx.enter_context(tc.tile_pool(name="ring", bufs=2))
        psum = ctx.enter_context(tc.psum_pool(name="psum", bufs=1))
        ctx.enter_context(tc.manual_schedule())

        planes = keep.tile([P, S_PLANE + L], U8, align_bytes=64)
        e_scales = keep.tile([P, B * D], U8, align_bytes=64)
        e_raw = keep.tile([P, B * D // 2], I32)
        mask_rows = keep.tile([P, P], BF16)
        ident = keep.tile([P, P], F32)
        sorter = keep.tile([P, P], F32)
        ident_bf = keep.tile([P, P], BF16)
        emb_in = keep.tile([P, D // P], BF16)
        bias_in = keep.tile([P, C // P], BF16)
        scale_in = keep.tile([P, 2, SLOTS], BF16)
        s_words = keep.tile([P, 2 * L], U8, align_bytes=64)
        e_words = keep.tile([P, 2 * B * D], U8, align_bytes=64)
        w_raw = [keep.tile([P, SLOTS, C], BF16, name="w_raw%d" % g) for g in range(2)]
        w_in = [keep.tile([P, C, SLOTS], BF16, align_bytes=64, tag="w_in%d" % g, name="w_in") for g in range(2)]
        w_codes = [keep.tile([P, C], U32, align_bytes=64, name="w_codes%d" % g) for g in range(2)]
        w_scales = [keep.tile([P, C], U8, align_bytes=64, name="w_scales%d" % g) for g in range(2)]
        tgt = [keep.tile([P, SLOTS, width], BF16, name="tgt%d" % k) for k, (g, c0, width) in enumerate(PIECES)]
        emb_all = keep.tile([P, D], BF16)
        bias_all = keep.tile([P, C + 6 * BIAS_WRAP], BF16)
        mask_col = keep.tile([P, L // P], F32)
        scale_col = keep.tile([P, 2 * SLOTS], F32)
        y_codes = [keep.tile([P, B * C], U32, align_bytes=64, name="y_codes%d" % g) for g in range(2)]
        y_scales = [keep.tile([P, B * C], U8, align_bytes=64, name="y_scales%d" % g) for g in range(2)]


        def load_scale_rows(source, col0, width):
            for quadrant in range(4):
                nc.sync.dma_start(
                    out=planes[32 * quadrant : 32 * quadrant + 4, col0 : col0 + width].bitcast(I32),
                    in_=source[0, 4 * quadrant : 4 * quadrant + 4, :].bitcast(I32),
                )

        def load_weight(g, u):
            rows = head_weight[GROUP * g : GROUP * (g + 1), :].rearrange("(q u r e) c -> u q r (e c)", u=2, r=8, e=2)
            nc.sync.dma_start(out=w_raw[g][:, 2 * u : 2 * u + 2, :].rearrange("p e c -> p (e c)"), in_=rows[u])

        def load_target(k, t0=0, t1=SLOTS):
            g, c0, width = PIECES[k]
            rows = target[GROUP * g : GROUP * (g + 1)].rearrange("(p t) r c -> p t (r c)", t=SLOTS)
            nc.sync.dma_start(out=tgt[k][:, t0:t1, :], in_=rows[:, t0:t1, c0 : c0 + width])

        nc.vector.memset(planes[:, 0:S_PLANE].bitcast(I32), 0)
        nc.vector.memset(mask_rows[:], 0.0)
        nc.vector.memset(planes[:, S_PLANE:].bitcast(I32), 0)
        make_identity(nc, ident[:])
        by_slot = ident[:].rearrange("p (j t) -> p t j", t=SLOTS)
        nc.gpsimd.tensor_tensor(
            out=sorter[:].rearrange("p (t j) -> p t j", t=SLOTS), in0=by_slot, in1=by_slot, op=ALU.mult
        )
        load_scale_rows(latent_scales, 0, S_PLANE)
        nc.sync.dma_start(out=bias_in[:], in_=head_bias.rearrange("(p j) -> p j", p=P))
        nc.sync.dma_start(out=emb_in[:], in_=mask_embedding.rearrange("(p j) -> p j", p=P))
        nc.sync.dma_start(out=mask_rows[0 : L // P, :], in_=mask.rearrange("(i p) -> i p", p=P))
        nc.sync.dma_start(out=e_raw[:], in_=latent_words[0].bitcast(I32))
        load_scale_rows(scatter_scales, S_PLANE, L)
        load_target(0, 0, 2)
        nc.sync.dma_start(out=s_words[:].bitcast(I32), in_=scatter_words[0].bitcast(I32))
        load_weight(0, 0)
        load_weight(0, 1)
        load_target(0, 2, SLOTS)
        load_target(1)
        load_weight(1, 0)
        load_weight(1, 1)
        nc.sync.dma_start(out=scale_in[:], in_=patch_scale.rearrange("(g p t) -> p g t", p=P, t=SLOTS))
        for k in range(2, len(PIECES)):
            load_target(k)


        def sort_columns(out, source, run):
            nc.vector.tensor_copy(
                out=out.rearrange("p (g u q x) -> p g u q x", u=2, q=16, x=run),
                in_=source.rearrange("p (g q u x) -> p g u q x", u=2, q=16, x=run),
            )

        def spread(bank, source, words):
            for w in range(words):
                column = source[:].bitcast(F32)[:, w : w + 1]
                nc.tensor.transpose(bank[:, P * w : P * (w + 1)], column.to_broadcast([P, P]), ident[:])

        nc.scalar.activation(out=ident_bf[:], in_=ident[:], func=ACT.Copy)
        sort_columns(e_scales[:].bitcast(I32), planes[:, 0:S_PLANE].bitcast(I32), 4)
        bias_bank = psum.tile([P, BANK], F32, tag="two2")
        spread(bias_bank, bias_in, 3)
        bias_words = bias_all[:].bitcast(F32).rearrange("p (q w) -> p q w", w=3)
        bias_turned = bias_bank[:, 0 : 3 * P].rearrange("p (w q) -> p q w", w=3)
        nc.scalar.copy(out=bias_words[:, 0:P, :], in_=bias_turned)
        nc.scalar.copy(out=bias_words[:, P : P + BIAS_WRAP, :], in_=bias_turned[:, 0:BIAS_WRAP, :])
        emb_bank = psum.tile([P, BANK], F32, tag="two0")
        spread(emb_bank, emb_in, 4)
        nc.scalar.copy(
            out=emb_all[:].bitcast(F32).rearrange("p (u b h w) -> p u b h w", u=2, h=2, w=4),
            in_=emb_bank[:].rearrange("p (w b u h) -> p u b h w", w=4, u=2, h=2),
        )
        for r in range(B):
            image = slice(D // 2 * r, D // 2 * (r + 1))
            sort_columns(e_words[:].bitcast(I32)[:, image], e_raw[:, image], 8)
        mask_bank = psum.tile([P, P], BF16, tag="two1")
        nc.tensor.transpose(mask_bank[:], mask_rows[:], ident_bf[:])
        nc.scalar.copy(out=mask_col[:], in_=mask_bank[:, 0 : L // P])


        def interleave_weight(g, chunk):
            cols = slice(CHUNK * chunk, CHUNK * (chunk + 1))
            nc.scalar.copy(
                out=w_in[g][:, cols, :].rearrange("p (c i) t -> p c t i", i=RUN),
                in_=w_raw[g][:, :, cols].rearrange("p t (c i) -> p c t i", i=RUN),
            )

        def quantize_weight(g):
            for c0, c1 in ((0, 512), (512, C)):
                nc.vector.quantize_mx(
                    out=w_codes[g][:, c0:c1].bitcast(FP8X4),
                    scales=w_scales[g][:, c0:c1],
                    in_=w_in[g][:, c0:c1, :].rearrange("p c t -> p (c t)"),
                )


        taken, mixed, h_rows, h_in, h_codes, h_scales = [], {}, {}, {}, {}, {}

        def stage_one_bank():
            tag = "one%d" % (len(taken) % STAGE_ONE_BANKS)
            taken.append(psum.tile([P, BANK], F32, tag=tag, name="stage_one_bank"))
            return taken[-1]

        def mix(m):
            unit, g = m // 8, m % 2
            l0 = GROUP * (unit // 2) + P * (m // 2 % 4)
            d0 = D * (unit % 2) + GROUP * g
            mixed[m] = stage_one_bank()
            nc.tensor.matmul_mx(
                out=mixed[m][:],
                lhsT=s_words[:, 2 * l0 : 2 * (l0 + P)].bitcast(FP4X4),
                lhsT_scale=planes[:, S_PLANE + l0 : S_PLANE + l0 + P],
                rhs=e_words[:, 2 * d0 : 2 * (d0 + GROUP)].bitcast(FP4X4),
                rhs_scale=e_scales[:, d0 : d0 + GROUP],
                start=True,
                stop=True,
            )

        def add_embedding(m):
            step, g = m // 2, m % 2
            if g == 0:
                h_rows[step] = ring.tile([P, D], BF16, tag="h_rows", bufs=4, name="h_rows")
            i = 4 * (m // 16) + step % 4
            nc.vector.scalar_tensor_tensor(
                out=h_rows[step][:, GROUP * g : GROUP * (g + 1)].rearrange("p (u x) -> p u x", u=2),
                in0=emb_all[:].rearrange("p (u g x) -> p u g x", u=2, g=2)[:, :, g, :],
                scalar=mask_col[:, i : i + 1],
                in1=mixed[m][:].rearrange("p (u x) -> p u x", u=2),
                op0=ALU.mult,
                op1=ALU.add,
            )

        def turn(step):
            unit = step // 4
            bank = stage_one_bank()
            rows = h_rows[step][:].bitcast(F32)
            for quarter in range(4):
                cols = slice(P * quarter, P * (quarter + 1))
                nc.tensor.transpose(bank[:, cols], rows[:, cols], sorter[:])
            if step % 4 == 0:
                h_in[unit] = keep.tile([P, 2 * GROUP * SLOTS], BF16, tag="h_in%d" % unit, align_bytes=64, name="h_in")
            laid = h_in[unit][:].bitcast(F32).rearrange("p (g t i j u) -> p g t i j u", g=2, t=SLOTS, i=4, u=2)
            nc.scalar.copy(
                out=laid[:, :, :, step % 4],
                in_=bank[:].rearrange("p (g u t j) -> p g t j u", g=2, u=2, t=SLOTS),
            )

        def quantize_h(unit):
            h_codes[unit] = ring.tile([P, 2 * GROUP], U32, tag="h_codes", align_bytes=64, name="h_codes")
            h_scales[unit] = ring.tile([P, 2 * GROUP], U8, tag="h_scales", align_bytes=64, name="h_scales")
            nc.vector.quantize_mx(out=h_codes[unit][:].bitcast(FP8X4), scales=h_scales[unit][:], in_=h_in[unit][:])


        offsets, summed, ys, y_in = {}, {}, {}, {}

        def place(j):
            if j < 2 * WIDE:
                return j // 2, range(2 * (j % 2), 2 * (j % 2) + 2)
            return j - WIDE, range(SLOTS)

        def subtract_target(engine, j, tag):
            k, slots = place(j)
            g, c0, width = PIECES[k]
            offsets[j] = keep.tile([P, len(slots), width], F32, tag=tag, align_bytes=64, name="offset")
            bias = bias_all[:, c0 % C : c0 % C + width].rearrange("p (o c) -> p o c", o=1)
            engine.tensor_tensor(
                out=offsets[j][:],
                in0=bias.to_broadcast([P, len(slots), width]),
                in1=tgt[k][:, slots.start : slots.stop, :],
                op=ALU.subtract,
            )

        def patch_scales(g, t):
            return scale_col[:, SLOTS * g + t : SLOTS * g + t + 1]

        def scale_offset(j):
            k, slots = place(j)
            for row, t in enumerate(slots):
                values = offsets[j][:, row, :]
                nc.scalar.activation(out=values, in_=values, func=ACT.Copy, scale=patch_scales(PIECES[k][0], t))

        def bank_rows(n):
            k, slots = place(n // 2)
            each = len(slots) // 2
            return k, slots, range(each * (n % 2), each * (n % 2 + 1))

        def predict(n):
            k, slots, rows = bank_rows(n)
            g, c0, width = PIECES[k]
            summed[n] = psum.tile([P, BANK], F32, tag="two%d" % (n % AHEAD), name="result_bank")
            cuts = [c0, C, c0 + width] if c0 < C < c0 + width else [c0, c0 + width]
            for at, row in enumerate(rows):
                for a, b in zip(cuts, cuts[1:]):
                    unit = 2 * g + a // C
                    pixels = slice(a % C, a % C + b - a)
                    for half in range(2):
                        first = GROUP * half + P * slots[row]
                        nc.tensor.matmul_mx(
                            out=summed[n][:, width * at + a - c0 : width * at + b - c0],
                            lhsT=h_codes[unit][:, first : first + P].bitcast(FP8X4),
                            lhsT_scale=h_scales[unit][:, first : first + P],
                            rhs=w_codes[half][:, pixels].bitcast(FP8X4),
                            rhs_scale=w_scales[half][:, pixels],
                            start=(half == 0),
                            stop=(half == 1),
                        )

        def finish(n):
            k, slots, rows = bank_rows(n)
            g, c0, width = PIECES[k]
            if k not in ys:
                ys[k] = ring.tile([P, SLOTS, width], F32, tag="y", bufs=4, name="y")
            for at, row in enumerate(rows):
                nc.vector.scalar_tensor_tensor(
                    out=ys[k][:, slots[row], :],
                    in0=summed[n][:, width * at : width * (at + 1)],
                    scalar=patch_scales(g, slots[row]),
                    in1=offsets[n // 2][:, row, :],
                    op0=ALU.mult,
                    op1=ALU.add,
                )
            if n % 2 == 1:
                stored = out_0[GROUP * g : GROUP * (g + 1)].rearrange("(p t) r c -> p t (r c)", t=SLOTS)
                nc.sync.dma_start(
                    out=stored[:, slots.start : slots.stop, c0 : c0 + width],
                    in_=ys[k][:, slots.start : slots.stop, :],
                )

        def interleave_y(copy, k):
            width = PIECES[k][2]
            y_in[k] = keep.tile([P, width, SLOTS], BF16, tag="y_in%d" % k, align_bytes=64, name="y_in")
            for c0 in range(0, width, CHUNK):
                copy(
                    out=y_in[k][:, c0 : c0 + CHUNK, :].rearrange("p (c i) t -> p c t i", i=RUN),
                    in_=ys[k][:, :, c0 : c0 + CHUNK].rearrange("p t (c i) -> p c t i", i=RUN),
                )

        def quantize_y(k):
            g, c0, width = PIECES[k]
            nc.vector.quantize_mx(
                out=y_codes[g][:, c0 : c0 + width].bitcast(FP8X4),
                scales=y_scales[g][:, c0 : c0 + width],
                in_=y_in[k][:].rearrange("p c t -> p (c t)"),
            )

        def store_codes(k0, k1):
            g, a, b = PIECES[k0][0], PIECES[k0][1], PIECES[k1][1] + PIECES[k1][2]
            stored = out_1[g].rearrange("p n t -> p (n t)")
            nc.sync.dma_start(out=stored[:, SLOTS * a : SLOTS * b].bitcast(I32), in_=y_codes[g][:, a:b].bitcast(I32))

        def store_scales(g):
            for quadrant in range(4):
                nc.sync.dma_start(
                    out=out_2[g, 4 * quadrant : 4 * quadrant + 4, :].bitcast(I32),
                    in_=y_scales[g][32 * quadrant : 32 * quadrant + 4, :].bitcast(I32),
                )


        def ahead_of_turn(step):
            if step < 6:
                interleave_weight(step // 3, step % 3)
            if step == SCALE_LAG:
                nc.scalar.copy(out=scale_col[:], in_=scale_in[:].rearrange("p g t -> p (g t)"))
            if step >= SCALE_LAG:
                scale_offset(step - SCALE_LAG)

        def behind_bank(n):
            if n % 4 == 3 and n // 4 < WIDE:
                interleave_y(nc.scalar.copy, n // 4)
                if BANK_ENDS[-2] <= n < BANK_ENDS[-1] - 1:
                    scale_offset(PART_ENDS[-1] - 1)

        def window(w, held):
            pass0, pass1 = PASS_ENDS[w - 1], PASS_ENDS[w]
            bank0, bank1 = BANK_ENDS[w - 1], BANK_ENDS[w]
            for j in range(PART_ENDS[w - 1], PART_ENDS[w]):
                subtract_target(nc.gpsimd, j, held if j == PART_ENDS[w - 1] else "offset%d" % j)
            fills = (pass0, pass1 - 3, pass1 - 2)
            for m in range(pass0, pass1):
                if m in fills:
                    predict(bank0 + fills.index(m))
                add_embedding(m)
                if m + AHEAD < pass1:
                    mix(m + AHEAD)
                if m % 2 == 1:
                    ahead_of_turn(m // 2)
                    turn(m // 2)
            for n in range(bank0, bank1):
                finish(n)
                if n + AHEAD < bank1:
                    predict(n + AHEAD)
                if n + AHEAD + 1 == bank1:
                    for m in range(pass1, min(pass1 + AHEAD, PASSES)):
                        mix(m)
                behind_bank(n)

        for m in range(AHEAD):
            mix(m)
        subtract_target(nc.vector, 0, "offset0")
        for j in range(1, PART_ENDS[0]):
            subtract_target(nc.gpsimd, j, "offset%d" % j)
        for m in range(PASS_ENDS[0]):
            add_embedding(m)
            mix(m + AHEAD)
            if m % 2 == 1:
                ahead_of_turn(m // 2)
                turn(m // 2)
        quantize_h(0)
        quantize_weight(0)
        quantize_weight(1)

        window(1, "w_in1")
        quantize_h(1)

        window(2, "h_in1")
        quantize_y(0)
        quantize_h(2)
        store_codes(0, 0)

        window(3, "h_in2")
        quantize_h(3)

        first, last_piece = BANK_ENDS[-1], len(PIECES) - 1
        for n in range(first, first + AHEAD):
            predict(n)
        quantize_y(1)
        quantize_y(2)
        store_codes(1, 2)
        store_scales(0)
        for n in range(first, RESULT_BANKS - 2):
            finish(n)
            if n + AHEAD < RESULT_BANKS:
                predict(n + AHEAD)
            behind_bank(n)
        interleave_y(nc.scalar.copy, last_piece - 1)
        quantize_y(3)
        store_codes(3, 3)
        finish(RESULT_BANKS - 2)
        finish(RESULT_BANKS - 1)
        quantize_y(4)
        interleave_y(nc.vector.tensor_copy, last_piece)
        quantize_y(last_piece - 1)
        store_codes(4, last_piece - 1)
        quantize_y(last_piece)
        store_codes(last_piece, last_piece)
        store_scales(1)
